import numpy as np
import ml_dtypes


def mxq(x, axis, fmt="e4m3"):
    dtype, down = {"e4m3": (ml_dtypes.float8_e4m3fn, 7), "e5m2": (ml_dtypes.float8_e5m2, 14)}[fmt]
    v = np.moveaxis(np.asarray(x, np.float32).astype(ml_dtypes.bfloat16).astype(np.float64), axis, -1)
    blocks = v.reshape(v.shape[:-1] + (-1, 32))
    amax = np.abs(blocks).max(-1, keepdims=True)
    byte = np.maximum(np.where(amax > 0, np.frexp(amax)[1] - 1 + 127, 0) - down, 1)
    scale = np.exp2(byte - 127.0)
    codes = (blocks / scale).astype(np.float32).astype(dtype).astype(np.float64)
    return np.moveaxis((codes * scale).reshape(v.shape), -1, axis)


WIDE = False


def mx_kscale(k):
    if not WIDE:
        return np.ones(k)
    levels = np.array([10, -10, 5, -5, 0])
    if k % 512:
        return np.exp2(np.random.permutation(np.resize(levels, k // 32))).repeat(32)
    a = np.empty((k // 512, 16))
    for p in range(k // 512):
        a[p, :8] = np.random.permutation(np.resize(levels, 8))
        for g in range(8):
            far = levels[np.abs(levels - a[p, g]) >= 10]
            a[p, g + 8] = far[np.random.randint(len(far))]
    return np.exp2(a.ravel()).repeat(32)


def f64(x):
    return np.asarray(x).astype(np.float64)


def striped(idx):
    return np.tile(idx.reshape(-1, 16).T, (8, 1)).astype(np.uint16)


def unstriped(offs):
    return offs[:16].T.reshape(-1).astype(np.int64)


E2M1 = np.array([0.0, 0.5, 1.0, 1.5, 2.0, 3.0, 4.0, 6.0, -0.0, -0.5, -1.0, -1.5, -2.0, -3.0, -4.0, -6.0])


def pack_fp4(w):
    k, n = w.shape
    w = f64(np.asarray(w, np.float32).astype(ml_dtypes.bfloat16)).reshape(k // 32, 32, n)
    amax = np.abs(w).max(1)
    mant, ex = np.frexp(amax / 6.0)
    byte = np.clip(np.where(amax > 0, np.where(mant > 0.5, ex, ex - 1) + 127, 1), 1, 254)
    scaled = (w * np.exp2(127.0 - byte)[:, None, :]).reshape(k, n).astype(np.float32)
    c = np.ascontiguousarray(scaled.reshape(k // 512, 128, 4, n).transpose(0, 1, 3, 2)).astype(ml_dtypes.float4_e2m1fn).view(np.uint8) & 0xF
    words = (c[..., 0::2] | (c[..., 1::2] << 4)).reshape(k // 512, 128, 2 * n)
    return np.ascontiguousarray(words), np.ascontiguousarray(byte.astype(np.uint8).reshape(k // 512, 16, n))


def unpack_fp4(words, scales):
    g, _, n = scales.shape
    words = np.ascontiguousarray(words).reshape(g, 128, n, 2)
    nib = np.empty((g, 128, n, 4), np.uint8)
    nib[..., 0::2] = words & 0xF
    nib[..., 1::2] = words >> 4
    vals = E2M1[nib] * np.repeat(np.exp2(scales.astype(np.float64) - 127.0), 8, axis=1)[..., None]
    return vals.transpose(0, 1, 3, 2).reshape(g * 512, n)


def relu(v):
    return np.maximum(v, 0.0)


K, T, S, V, H, N = 512, 1024, 512, 256, 512, 256


def setup_inputs():
    n = np.random.standard_normal
    s = mx_kscale(K)[:, None]
    u = mx_kscale(H)
    packed_w3 = pack_fp4(n((H, N)) / np.sqrt(H) / u[:, None])
    return {
        "xT": (n((K, T)) * s).astype(np.float32),
        "w1": (n((K, H)) / np.sqrt(2 * K) / s * u).astype(np.float32),
        "w2": (n((K, H)) / np.sqrt(2 * K) / s * u).astype(np.float32),
        "w3_words": packed_w3[0],
        "w3_scales": packed_w3[1],
        "offs": striped(np.random.permutation(T)[:S]),
        "cen": striped(np.random.permutation(S)[:V]),
        "pos1": striped(np.random.permutation(S)[:V]),
        "pos2": striped(np.random.permutation(S)[:V]),
        "pos3": striped(np.random.permutation(S)[:V]),
    }


def reference(xT, w1, w2, w3_words, w3_scales, offs, cen, pos1, pos2, pos3):
    xq = mxq(f64(xT)[:, unstriped(offs)], 0, "e4m3")
    y = mxq(f64(w1), 0, "e4m3").T @ xq
    yc = y[:, unstriped(cen)]
    e = mxq(f64(w2), 0, "e4m3").T @ xq
    z = np.maximum(np.maximum(relu(yc + e[:, unstriped(pos1)]), relu(yc + e[:, unstriped(pos2)])), relu(yc + e[:, unstriped(pos3)]))
    return unpack_fp4(w3_words, w3_scales).T @ mxq(z, 0, "e4m3")

@@ -1,0 +1,168 @@
+from contextlib import ExitStack
+
+import concourse.mybir as mybir
+
+K, T, S, V, H, N = 512, 1024, 512, 256, 512, 256
+FLOPS = 2 * (2 * K * H * S + H * N * V)
+
+F32 = mybir.dt.float32
+BF16 = mybir.dt.bfloat16
+I32 = mybir.dt.int32
+U32 = mybir.dt.uint32
+U16 = mybir.dt.uint16
+U8 = mybir.dt.uint8
+FP8X4 = mybir.dt.float8_e4m3fn_x4
+FP4X4 = mybir.dt.float4_e2m1fn_x4
+ALU = mybir.AluOpType
+ACT = mybir.ActivationFunctionType
+
+P = 128
+PACK = 4
+HALF = V // 2
+
+
+def tile_picked_edgecv_relu_e_kernel(tc, xT, w1, w2, w3_words, w3_scales, offs, cen, pos1, pos2, pos3, out):
+    nc = tc.nc
+    with ExitStack() as ctx:
+        lists = ctx.enter_context(tc.tile_pool(name="lists", bufs=1))
+        keep = ctx.enter_context(tc.tile_pool(name="keep", bufs=1))
+        acc_pool = ctx.enter_context(tc.psum_pool(name="acc", bufs=5))
+        out_pool = ctx.enter_context(tc.psum_pool(name="oacc", bufs=3))
+
+        def load_list(src, n, name):
+            t = lists.tile([P, n // 16], U16, name=name)
+            nc.sync.dma_start(t[:], src)
+            return t
+
+        x_rows = xT.rearrange("(p j) t -> p j t", j=PACK)
+        planes = [keep.tile([P, T], F32, name=f"xplane{j}") for j in range(PACK)]
+        nc.sync.dma_start(planes[0][:], x_rows[:, 0, :])
+        offs_t = load_list(offs, S, "offs_t")
+        for j in range(1, PACK):
+            nc.sync.dma_start(planes[j][:], x_rows[:, j, :])
+
+        def load_w(w, name):
+            rows = w.rearrange("(p j) c -> p j c", j=PACK)
+            pairs = []
+            for u in range(2):
+                t = keep.tile([P, 2, H], F32, name=f"{name}_raw{u}")
+                nc.sync.dma_start(t[:], rows[:, 2 * u : 2 * u + 2, :])
+                pairs.append(t)
+            return pairs
+
+        w2_raw = load_w(w2, "w2")
+        pos_t = [load_list(src, V, f"pos_t{d}") for d, src in enumerate((pos1, pos2, pos3))]
+        w1_raw = load_w(w1, "w1")
+        cen_t = load_list(cen, V, "cen_t")
+        w3w = keep.tile([P, 2 * N], U8, name="w3w", align_bytes=64)
+        nc.sync.dma_start(w3w[:].bitcast(I32), w3_words[0].bitcast(I32))
+        w3s = keep.tile([P, N], U8, name="w3s", align_bytes=64)
+        nc.gpsimd.memset(w3s[:], 0)
+        for q in range(4):
+            nc.sync.dma_start(w3s[32 * q : 32 * q + 4, :].bitcast(I32), w3_scales[0, 4 * q : 4 * q + 4, :].bitcast(I32))
+
+        warm = keep.tile([P, 2], F32, name="warm")
+        nc.gpsimd.memset(warm[:, 0:1], 0.0)
+        nc.scalar.activation(warm[:, 1:2], warm[:, 0:1], ACT.Relu)
+
+        xg = keep.tile([P, S, PACK], BF16, name="xg", align_bytes=64)
+        g01 = keep.tile([P, 2, S], F32, name="g01")
+        for j in range(2):
+            nc.vector.tensor_copy(g01[:, j, :], planes[j][:].indirect(offs_t[:]))
+        nc.scalar.copy(xg[:, :, 0:2], g01[:].rearrange("p j s -> p s j"))
+        for j in range(2, PACK):
+            nc.vector.tensor_copy(xg[:, :, j], planes[j][:].indirect(offs_t[:]))
+        xq = keep.tile([P, S], U32, name="xq", align_bytes=64)
+        xs = keep.tile([P, S], U8, name="xs", align_bytes=64)
+        nc.vector.quantize_mx(out=xq[:].bitcast(FP8X4), scales=xs[:], in_=xg[:].rearrange("p s j -> p (s j)"))
+
+        def cast(engine_copy, wg, raw, u, ts):
+            engine_copy(
+                wg[:, ts, :, 2 * u : 2 * u + 2].rearrange("p t m j -> p m t j"),
+                raw[u][:].rearrange("p j (m t) -> p m t j", t=PACK)[:, :, ts, :],
+            )
+
+        def quantise(wg, ts, name):
+            n = ts.stop - ts.start
+            wq = keep.tile([P, n * P], U32, name=f"{name}_q{ts.start}", align_bytes=64)
+            ws = keep.tile([P, n * P], U8, name=f"{name}_s{ts.start}", align_bytes=64)
+            nc.vector.quantize_mx(out=wq[:].bitcast(FP8X4), scales=ws[:], in_=wg[:, ts].rearrange("p t m j -> p (t m j)"))
+            return [(wq[:, i * P : (i + 1) * P], ws[:, i * P : (i + 1) * P]) for i in range(n)]
+
+        def product(op, name, pieces):
+            r = keep.tile([P, S], F32, name=name)
+            width = S // pieces
+            for i in range(pieces):
+                cols = slice(i * width, (i + 1) * width)
+                acc = acc_pool.tile([P, S], F32, name="acc")
+                nc.tensor.matmul_mx(out=acc[:, 0:width], lhsT=op[0].bitcast(FP8X4), lhsT_scale=op[1], rhs=xq[:, cols].bitcast(FP8X4), rhs_scale=xs[:, cols], start=True, stop=True)
+                nc.scalar.copy(r[:, cols], acc[:, 0:width])
+            return r
+
+        w2g = keep.tile([P, PACK, P, PACK], BF16, name="w2g", align_bytes=64)
+        cast(nc.scalar.copy, w2g, w2_raw, 0, slice(0, 4))
+        cast(nc.scalar.copy, w2g, w2_raw, 1, slice(0, 1))
+        ops = quantise(w2g, slice(0, 1), "w2")
+        e = [product(ops[0], "e0", 2)]
+        cast(nc.vector.tensor_copy, w2g, w2_raw, 1, slice(1, 4))
+        ops = quantise(w2g, slice(1, 2), "w2") + quantise(w2g, slice(2, 4), "w2")
+        for t in range(1, PACK):
+            e.append(product(ops[t - 1], f"e{t}", 1))
+        g = [keep.tile([P, PACK, V], F32, name=f"g{d}") for d in range(3)]
+        m12 = keep.tile([P, PACK, V], F32, name="m12")
+        m = keep.tile([P, PACK, V], F32, name="m")
+        for t in range(PACK):
+            for d in range(3):
+                nc.vector.tensor_copy(g[d][:, t, :], e[t][:].indirect(pos_t[d][:]))
+        w1g = keep.tile([P, PACK, P, PACK], BF16, name="w1g", align_bytes=64)
+        for u in range(2):
+            cast(nc.scalar.copy, w1g, w1_raw, u, slice(0, 4))
+        ops = quantise(w1g, slice(0, 4), "w1")
+        y = [product(ops[t], f"y{t}", 1) for t in range(PACK)]
+        nc.vector.tensor_tensor(m12[:], g[0][:], g[1][:], ALU.max)
+        nc.vector.tensor_tensor(m[:], m12[:], g[2][:], ALU.max)
+
+        out_v = out.rearrange("(a p) v -> p a v", p=P)
+        for h in range(2):
+            cols = slice(h * HALF, (h + 1) * HALF)
+            s = keep.tile([P, PACK, HALF], F32, name=f"s{h}")
+            for t in range(PACK):
+                nc.vector.tensor_tensor(s[:, t, :], y[t][:].indirect(cen_t[:, h * 8 : (h + 1) * 8]), m[:, t, cols], ALU.add)
+            z = keep.tile([P, HALF, PACK], BF16, name=f"z{h}", align_bytes=64)
+            if h == 0:
+                nc.scalar.activation(z[:], s[:].rearrange("p t v -> p v t"), ACT.Relu)
+            else:
+                nc.scalar.activation(z[:, :, 0:2], s[:, 0:2, :].rearrange("p t v -> p v t"), ACT.Relu)
+                nc.vector.tensor_scalar(z[:, :, 2:4], s[:, 2:4, :].rearrange("p t v -> p v t"), 0.0, None, ALU.max)
+            zq = keep.tile([P, HALF], U32, name=f"zq{h}", align_bytes=64)
+            zs = keep.tile([P, HALF], U8, name=f"zs{h}", align_bytes=64)
+            nc.vector.quantize_mx(out=zq[:].bitcast(FP8X4), scales=zs[:], in_=z[:].rearrange("p v t -> p (v t)"))
+            def project(dst, a):
+                nc.tensor.matmul_mx(
+                    out=dst,
+                    lhsT=w3w[:, 2 * P * a : 2 * P * (a + 1)].bitcast(FP4X4),
+                    lhsT_scale=w3s[:, P * a : P * (a + 1)],
+                    rhs=zq[:].bitcast(FP8X4),
+                    rhs_scale=zs[:],
+                    start=True,
+                    stop=True,
+                )
+
+            if h == 0:
+                oacc = out_pool.tile([P, 2, HALF], F32, name="oacc")
+                for a in range(2):
+                    project(oacc[:, a, :], a)
+                o = keep.tile([P, 2, HALF], F32, name="o0")
+                nc.scalar.copy(o[:], oacc[:])
+                nc.sync.dma_start(out_v[:, :, cols], o[:])
+            else:
+                for a in range(2):
+                    oacc = out_pool.tile([P, 2, HALF], F32, name="oacc")
+                    project(oacc[:, 0, :], a)
+                    o = keep.tile([P, HALF], F32, name=f"o1{a}")
+                    if a == 0:
+                        nc.vector.tensor_copy(o[:], oacc[:, 0, :])
+                        nc.sync.dma_start(out_v[:, a, cols], o[:])
+                    else:
+                        nc.scalar.copy(o[:], oacc[:, 0, :])
+                        nc.scalar.dma_start(out_v[:, a, cols], o[:])

@@ -42,55 +42,62 @@ def tile_picked_edgecv_relu_e_kernel(tc, xT, w1, w2, w3_words, w3_scales, offs, 
             nc.sync.dma_start(planes[j][:], x_rows[:, j, :])
 
         def load_w(w, name):
-            rows = w.rearrange("(p j) c -> p j c", j=PACK)
-            pairs = []
-            for u in range(2):
-                t = keep.tile([P, 2, H], F32, name=f"{name}_raw{u}")
-                nc.sync.dma_start(t[:], rows[:, 2 * u : 2 * u + 2, :])
-                pairs.append(t)
-            return pairs
+            t = keep.tile([P, PACK, H], F32, name=f"{name}_raw", tag=f"{name}_raw")
+            nc.sync.dma_start(t[:], w.rearrange("(p j) c -> p j c", j=PACK))
+            return t
 
-        w2_raw = load_w(w2, "w2")
+        w2_raw = keep.tile([P, PACK, H], F32, name="w2_raw")
+        for u in range(2):
+            nc.sync.dma_start(w2_raw[:, 2 * u : 2 * u + 2, :], w2.rearrange("(p j) c -> p j c", j=PACK)[:, 2 * u : 2 * u + 2, :])
         pos_t = [load_list(src, V, f"pos_t{d}") for d, src in enumerate((pos1, pos2, pos3))]
         w1_raw = load_w(w1, "w1")
         cen_t = load_list(cen, V, "cen_t")
         w3w = keep.tile([P, 2 * N], U8, name="w3w", align_bytes=64)
         nc.sync.dma_start(w3w[:].bitcast(I32), w3_words[0].bitcast(I32))
         w3s = keep.tile([P, N], U8, name="w3s", align_bytes=64)
-        nc.gpsimd.memset(w3s[:], 0)
+        nc.vector.memset(w3s[:].bitcast(I32), 0)
         for q in range(4):
             nc.sync.dma_start(w3s[32 * q : 32 * q + 4, :].bitcast(I32), w3_scales[0, 4 * q : 4 * q + 4, :].bitcast(I32))
 
         warm = keep.tile([P, 2], F32, name="warm")
-        nc.gpsimd.memset(warm[:, 0:1], 0.0)
+        nc.vector.memset(warm[:, 0:1], 0.0)
         nc.scalar.activation(warm[:, 1:2], warm[:, 0:1], ACT.Relu)
 
-        xg = keep.tile([P, S, PACK], BF16, name="xg", align_bytes=64)
+        SH = S // 2
+        xg = [keep.tile([P, SH, PACK], BF16, name=f"xg{h}", align_bytes=64) for h in range(2)]
         g01 = keep.tile([P, 2, S], F32, name="g01")
+        g23 = [keep.tile([P, 2, SH], F32, name=f"g23{h}") for h in range(2)]
         for j in range(2):
             nc.vector.tensor_copy(g01[:, j, :], planes[j][:].indirect(offs_t[:]))
-        nc.scalar.copy(xg[:, :, 0:2], g01[:].rearrange("p j s -> p s j"))
-        for j in range(2, PACK):
-            nc.vector.tensor_copy(xg[:, :, j], planes[j][:].indirect(offs_t[:]))
+        for h in range(2):
+            nc.scalar.copy(xg[h][:, :, 0:2], g01[:, :, h * SH : (h + 1) * SH].rearrange("p j s -> p s j"))
+        for j in range(2):
+            for h in range(2):
+                nc.vector.tensor_copy(g23[h][:, j, :], planes[2 + j][:].indirect(offs_t[:, h * 16 : (h + 1) * 16]))
+        nc.scalar.copy(xg[0][:, :, 2:4], g23[0][:].rearrange("p j s -> p s j"))
+        nc.vector.tensor_copy(xg[1][:, :, 2:4], g23[1][:].rearrange("p j s -> p s j"))
         xq = keep.tile([P, S], U32, name="xq", align_bytes=64)
         xs = keep.tile([P, S], U8, name="xs", align_bytes=64)
-        nc.vector.quantize_mx(out=xq[:].bitcast(FP8X4), scales=xs[:], in_=xg[:].rearrange("p s j -> p (s j)"))
+        for h in range(2):
+            cols = slice(h * SH, (h + 1) * SH)
+            nc.vector.quantize_mx(out=xq[:, cols].bitcast(FP8X4), scales=xs[:, cols], in_=xg[h][:].rearrange("p s j -> p (s j)"))
 
-        def cast(engine_copy, wg, raw, u, ts):
-            engine_copy(
-                wg[:, ts, :, 2 * u : 2 * u + 2].rearrange("p t m j -> p m t j"),
-                raw[u][:].rearrange("p j (m t) -> p m t j", t=PACK)[:, :, ts, :],
-            )
-
-        def quantise(wg, ts, name):
+        def cast(engine_copy, raw, ts, name):
             n = ts.stop - ts.start
-            wq = keep.tile([P, n * P], U32, name=f"{name}_q{ts.start}", align_bytes=64)
-            ws = keep.tile([P, n * P], U8, name=f"{name}_s{ts.start}", align_bytes=64)
-            nc.vector.quantize_mx(out=wq[:].bitcast(FP8X4), scales=ws[:], in_=wg[:, ts].rearrange("p t m j -> p (t m j)"))
+            wg = keep.tile([P, n, P, PACK], BF16, name=f"{name}_g{ts.start}", align_bytes=64)
+            engine_copy(
+                wg[:].rearrange("p t m j -> p m t j"),
+                raw[:].rearrange("p j (m t) -> p m t j", t=PACK)[:, :, ts, :],
+            )
+            return wg
+
+        def quantise(wg, n, name):
+            wq = keep.tile([P, n * P], U32, name=f"{name}_q", align_bytes=64)
+            ws = keep.tile([P, n * P], U8, name=f"{name}_s", align_bytes=64)
+            nc.vector.quantize_mx(out=wq[:].bitcast(FP8X4), scales=ws[:], in_=wg[:].rearrange("p t m j -> p (t m j)"))
             return [(wq[:, i * P : (i + 1) * P], ws[:, i * P : (i + 1) * P]) for i in range(n)]
 
-        def product(op, name, pieces):
-            r = keep.tile([P, S], F32, name=name)
+        def product(op, r, pieces):
             width = S // pieces
             for i in range(pieces):
                 cols = slice(i * width, (i + 1) * width)
@@ -99,35 +106,40 @@ def tile_picked_edgecv_relu_e_kernel(tc, xT, w1, w2, w3_words, w3_scales, offs, 
                 nc.scalar.copy(r[:, cols], acc[:, 0:width])
             return r
 
-        w2g = keep.tile([P, PACK, P, PACK], BF16, name="w2g", align_bytes=64)
-        cast(nc.scalar.copy, w2g, w2_raw, 0, slice(0, 4))
-        cast(nc.scalar.copy, w2g, w2_raw, 1, slice(0, 1))
-        ops = quantise(w2g, slice(0, 1), "w2")
-        e = [product(ops[0], "e0", 2)]
-        cast(nc.vector.tensor_copy, w2g, w2_raw, 1, slice(1, 4))
-        ops = quantise(w2g, slice(1, 2), "w2") + quantise(w2g, slice(2, 4), "w2")
-        for t in range(1, PACK):
-            e.append(product(ops[t - 1], f"e{t}", 1))
+        wg0 = keep.tile([P, 1, P, PACK], BF16, name="w2_one", tag="w2_one", align_bytes=64)
+        w2_dealt = w2_raw[:].rearrange("p j (m t) -> p m t j", t=PACK)
+        for u in range(2):
+            nc.scalar.copy(wg0[:, 0, :, 2 * u : 2 * u + 2], w2_dealt[:, :, 0, 2 * u : 2 * u + 2])
+        ops = quantise(wg0, 1, "w2a")
+        wg23 = cast(nc.scalar.copy, w2_raw, slice(2, 4), "w2")
+        wg1 = keep.tile([P, 1, P, PACK], BF16, name="w2_one", tag="w2_one", align_bytes=64)
+        nc.vector.tensor_copy(wg1[:, 0], w2_dealt[:, :, 1, :])
+        e = [product(ops[0], keep.tile([P, S], F32, name="e0")[:], 2)]
+        ops = quantise(wg1, 1, "w2b") + quantise(wg23, 2, "w2c")
         g = [keep.tile([P, PACK, V], F32, name=f"g{d}") for d in range(3)]
         m12 = keep.tile([P, PACK, V], F32, name="m12")
         m = keep.tile([P, PACK, V], F32, name="m")
+        e.append(product(ops[0], keep.tile([P, S], F32, name="e1")[:], 1))
+        w1g = cast(nc.scalar.copy, w1_raw, slice(0, 4), "w1")
+        w1ops = quantise(w1g, 4, "w1")
+        e23 = keep.tile([P, 2 * S], F32, name="e23", tag="w1_raw")
+        e.append(product(ops[1], e23[:, 0:S], 1))
+        e.append(product(ops[2], e23[:, S : 2 * S], 1))
+        y = [product(w1ops[t], keep.tile([P, S], F32, name=f"y{t}")[:], 1) for t in range(PACK)]
         for t in range(PACK):
             for d in range(3):
-                nc.vector.tensor_copy(g[d][:, t, :], e[t][:].indirect(pos_t[d][:]))
-        w1g = keep.tile([P, PACK, P, PACK], BF16, name="w1g", align_bytes=64)
-        for u in range(2):
-            cast(nc.scalar.copy, w1g, w1_raw, u, slice(0, 4))
-        ops = quantise(w1g, slice(0, 4), "w1")
-        y = [product(ops[t], f"y{t}", 1) for t in range(PACK)]
-        nc.vector.tensor_tensor(m12[:], g[0][:], g[1][:], ALU.max)
-        nc.vector.tensor_tensor(m[:], m12[:], g[2][:], ALU.max)
+                nc.vector.tensor_copy(g[d][:, t, :], e[t].indirect(pos_t[d][:]))
+        for ts in (slice(0, 2), slice(2, 4)):
+            nc.vector.tensor_tensor(m12[:, ts, :], g[0][:, ts, :], g[1][:, ts, :], ALU.max)
+        for ts in (slice(0, 2), slice(2, 4)):
+            nc.vector.tensor_tensor(m[:, ts, :], m12[:, ts, :], g[2][:, ts, :], ALU.max)
 
         out_v = out.rearrange("(a p) v -> p a v", p=P)
         for h in range(2):
             cols = slice(h * HALF, (h + 1) * HALF)
             s = keep.tile([P, PACK, HALF], F32, name=f"s{h}")
             for t in range(PACK):
-                nc.vector.tensor_tensor(s[:, t, :], y[t][:].indirect(cen_t[:, h * 8 : (h + 1) * 8]), m[:, t, cols], ALU.add)
+                nc.vector.tensor_tensor(s[:, t, :], y[t].indirect(cen_t[:, h * 8 : (h + 1) * 8]), m[:, t, cols], ALU.add)
             z = keep.tile([P, HALF, PACK], BF16, name=f"z{h}", align_bytes=64)
             if h == 0:
                 nc.scalar.activation(z[:], s[:].rearrange("p t v -> p v t"), ACT.Relu)

@@ -1,6 +1,7 @@
 from contextlib import ExitStack
 
 import concourse.mybir as mybir
+from concourse.masks import make_identity
 
 K, T, S, V, H, N = 512, 1024, 512, 256, 512, 256
 FLOPS = 2 * (2 * K * H * S + H * N * V)
@@ -26,8 +27,7 @@ def tile_picked_edgecv_relu_e_kernel(tc, xT, w1, w2, w3_words, w3_scales, offs, 
     with ExitStack() as ctx:
         lists = ctx.enter_context(tc.tile_pool(name="lists", bufs=1))
         keep = ctx.enter_context(tc.tile_pool(name="keep", bufs=1))
-        acc_pool = ctx.enter_context(tc.psum_pool(name="acc", bufs=5))
-        out_pool = ctx.enter_context(tc.psum_pool(name="oacc", bufs=3))
+        psum = ctx.enter_context(tc.psum_pool(name="psum", bufs=1))
 
         def load_list(src, n, name):
             t = lists.tile([P, n // 16], U16, name=name)
@@ -63,6 +63,9 @@ def tile_picked_edgecv_relu_e_kernel(tc, xT, w1, w2, w3_words, w3_scales, offs, 
         nc.vector.memset(warm[:, 0:1], 0.0)
         nc.scalar.activation(warm[:, 1:2], warm[:, 0:1], ACT.Relu)
 
+        ident = keep.tile([P, P], F32, name="ident")
+        make_identity(nc, ident[:])
+
         SH = S // 2
         xg = [keep.tile([P, SH, PACK], BF16, name=f"xg{h}", align_bytes=64) for h in range(2)]
         g01 = keep.tile([P, 2, S], F32, name="g01")
@@ -97,55 +100,88 @@ def tile_picked_edgecv_relu_e_kernel(tc, xT, w1, w2, w3_words, w3_scales, offs, 
             nc.vector.quantize_mx(out=wq[:].bitcast(FP8X4), scales=ws[:], in_=wg[:].rearrange("p t m j -> p (t m j)"))
             return [(wq[:, i * P : (i + 1) * P], ws[:, i * P : (i + 1) * P]) for i in range(n)]
 
-        def product(op, r, pieces):
-            width = S // pieces
-            for i in range(pieces):
+        def product(op, r, banks):
+            width = S // len(banks)
+            for i, bank in enumerate(banks):
                 cols = slice(i * width, (i + 1) * width)
-                acc = acc_pool.tile([P, S], F32, name="acc")
+                acc = psum.tile([P, S], F32, name=bank, tag=bank)
                 nc.tensor.matmul_mx(out=acc[:, 0:width], lhsT=op[0].bitcast(FP8X4), lhsT_scale=op[1], rhs=xq[:, cols].bitcast(FP8X4), rhs_scale=xs[:, cols], start=True, stop=True)
                 nc.scalar.copy(r[:, cols], acc[:, 0:width])
             return r
+
+        def row_tile(name, tag=None):
+            return keep.tile([P, S], F32, name=name, tag=tag or name)[:]
 
         wg0 = keep.tile([P, 1, P, PACK], BF16, name="w2_one", tag="w2_one", align_bytes=64)
         w2_dealt = w2_raw[:].rearrange("p j (m t) -> p m t j", t=PACK)
         for u in range(2):
             nc.scalar.copy(wg0[:, 0, :, 2 * u : 2 * u + 2], w2_dealt[:, :, 0, 2 * u : 2 * u + 2])
         ops = quantise(wg0, 1, "w2a")
-        wg23 = cast(nc.scalar.copy, w2_raw, slice(2, 4), "w2")
-        wg1 = keep.tile([P, 1, P, PACK], BF16, name="w2_one", tag="w2_one", align_bytes=64)
-        nc.vector.tensor_copy(wg1[:, 0], w2_dealt[:, :, 1, :])
-        e = [product(ops[0], keep.tile([P, S], F32, name="e0")[:], 2)]
+        wg1 = cast(nc.scalar.copy, w2_raw, slice(1, 2), "w2")
+        wg23 = keep.tile([P, 2, P, PACK], BF16, name="w2_one", tag="w2_one", align_bytes=64)
+        nc.vector.tensor_copy(wg23[:].rearrange("p t m j -> p m t j"), w2_dealt[:, :, 2:4, :])
+        e = [product(ops[0], row_tile("e0"), ["a0", "a1"])]
         ops = quantise(wg1, 1, "w2b") + quantise(wg23, 2, "w2c")
         g = [keep.tile([P, PACK, V], F32, name=f"g{d}") for d in range(3)]
-        m12 = keep.tile([P, PACK, V], F32, name="m12")
-        m = keep.tile([P, PACK, V], F32, name="m")
-        e.append(product(ops[0], keep.tile([P, S], F32, name="e1")[:], 1))
+        e.append(product(ops[0], row_tile("e1"), ["a2"]))
         w1g = cast(nc.scalar.copy, w1_raw, slice(0, 4), "w1")
         w1ops = quantise(w1g, 4, "w1")
-        e23 = keep.tile([P, 2 * S], F32, name="e23", tag="w1_raw")
-        e.append(product(ops[1], e23[:, 0:S], 1))
-        e.append(product(ops[2], e23[:, S : 2 * S], 1))
-        y = [product(w1ops[t], keep.tile([P, S], F32, name=f"y{t}")[:], 1) for t in range(PACK)]
-        for t in range(PACK):
+        e.append(product(ops[1], row_tile("e2", "w1_raw"), ["a3"]))
+        y = [product(w1ops[t], row_tile(f"y{t}"), [f"a{t}"]) for t in range(2)]
+        e.append(product(ops[2], row_tile("e3"), ["a0"]))
+        y.append(product(w1ops[2], row_tile("y2"), ["a1"]))
+        edge = [psum.tile([P, 2, 2, P], F32, name=f"edge{d}", tag=f"edge{d}") for d in range(3)]
+
+        def turn(d, t, src, first, last):
+            for h in range(2):
+                nc.tensor.matmul(edge[d][:, t, h, :], lhsT=src[:, t, h * HALF : (h + 1) * HALF], rhs=ident[:], is_transpose=True, start=first and h == 0, stop=last and h == 1)
+
+        def fetch(t):
             for d in range(3):
                 nc.vector.tensor_copy(g[d][:, t, :], e[t].indirect(pos_t[d][:]))
-        for ts in (slice(0, 2), slice(2, 4)):
-            nc.vector.tensor_tensor(m12[:, ts, :], g[0][:, ts, :], g[1][:, ts, :], ALU.max)
-        for ts in (slice(0, 2), slice(2, 4)):
-            nc.vector.tensor_tensor(m[:, ts, :], m12[:, ts, :], g[2][:, ts, :], ALU.max)
+
+        for t in range(3):
+            fetch(t)
+        for t in range(2):
+            for d in range(3):
+                turn(d, t, g[d], t == 0, False)
+        yc = keep.tile([P, 2, V], F32, name="yc")
+        for t in range(2):
+            nc.vector.tensor_copy(yc[:, t, :], y[t].indirect(cen_t[:]))
+        r = []
+        for d in range(3):
+            for t in range(2):
+                turn(d, t, yc, False, t == 1)
+            rd = keep.tile([P, 4 * P], BF16, name=f"r{d}", tag=f"r{d}")
+            nc.scalar.activation(rd[:].rearrange("v (h p t) -> v h p t", h=2, t=2), edge[d][:].rearrange("v t h p -> v h p t"), ACT.Relu)
+            r.append(rd)
+        y.append(product(w1ops[3], row_tile("y3"), ["edge0"]))
+        fetch(3)
+        m12 = keep.tile([P, 2, V], F32, name="m12")
+        nc.vector.tensor_tensor(m12[:], g[0][:, 2:4, :], g[1][:, 2:4, :], ALU.max)
+        r12 = keep.tile([P, 4 * P], BF16, name="r12", tag="r12")
+        nc.vector.tensor_tensor(r12[:], r[0][:], r[1][:], ALU.max)
+        m = keep.tile([P, 2, V], F32, name="m", tag="r0")
+        nc.vector.tensor_tensor(m[:], m12[:], g[2][:, 2:4, :], ALU.max)
+        zt = keep.tile([P, 4 * P], BF16, name="zt")
+        nc.vector.tensor_tensor(zt[:], r12[:], r[2][:], ALU.max)
+        zs_in = [keep.tile([P, HALF, PACK], BF16, name=f"z{h}", align_bytes=64) for h in range(2)]
+        for h in range(2):
+            back = psum.tile([P, HALF], F32, name=f"a{h}", tag=f"a{h}")
+            nc.tensor.transpose(back[:], zt[:, 2 * P * h : 2 * P * (h + 1)].bitcast(F32), ident[:])
+            nc.scalar.copy(zs_in[h][:, :, 0:2], back[:].bitcast(BF16).rearrange("p (v t) -> p v t", t=2))
 
         out_v = out.rearrange("(a p) v -> p a v", p=P)
         for h in range(2):
             cols = slice(h * HALF, (h + 1) * HALF)
-            s = keep.tile([P, PACK, HALF], F32, name=f"s{h}")
-            for t in range(PACK):
-                nc.vector.tensor_tensor(s[:, t, :], y[t].indirect(cen_t[:, h * 8 : (h + 1) * 8]), m[:, t, cols], ALU.add)
-            z = keep.tile([P, HALF, PACK], BF16, name=f"z{h}", align_bytes=64)
+            s = keep.tile([P, 2, HALF], F32, name=f"s{h}", tag=("r2", "r12")[h])
+            for t in range(2):
+                nc.vector.tensor_tensor(s[:, t, :], y[2 + t].indirect(cen_t[:, h * 8 : (h + 1) * 8]), m[:, t, cols], ALU.add)
+            z = zs_in[h]
             if h == 0:
-                nc.scalar.activation(z[:], s[:].rearrange("p t v -> p v t"), ACT.Relu)
+                nc.scalar.activation(z[:, :, 2:4], s[:].rearrange("p t v -> p v t"), ACT.Relu)
             else:
-                nc.scalar.activation(z[:, :, 0:2], s[:, 0:2, :].rearrange("p t v -> p v t"), ACT.Relu)
-                nc.vector.tensor_scalar(z[:, :, 2:4], s[:, 2:4, :].rearrange("p t v -> p v t"), 0.0, None, ALU.max)
+                nc.vector.tensor_scalar(z[:, :, 2:4], s[:].rearrange("p t v -> p v t"), 0.0, None, ALU.max)
             zq = keep.tile([P, HALF], U32, name=f"zq{h}", align_bytes=64)
             zs = keep.tile([P, HALF], U8, name=f"zs{h}", align_bytes=64)
             nc.vector.quantize_mx(out=zq[:].bitcast(FP8X4), scales=zs[:], in_=z[:].rearrange("p v t -> p (v t)"))
@@ -161,7 +197,7 @@ def tile_picked_edgecv_relu_e_kernel(tc, xT, w1, w2, w3_words, w3_scales, offs, 
                 )
 
             if h == 0:
-                oacc = out_pool.tile([P, 2, HALF], F32, name="oacc")
+                oacc = psum.tile([P, 2, HALF], F32, name="a2", tag="a2")
                 for a in range(2):
                     project(oacc[:, a, :], a)
                 o = keep.tile([P, 2, HALF], F32, name="o0")
@@ -169,7 +205,7 @@ def tile_picked_edgecv_relu_e_kernel(tc, xT, w1, w2, w3_words, w3_scales, offs, 
                 nc.sync.dma_start(out_v[:, :, cols], o[:])
             else:
                 for a in range(2):
-                    oacc = out_pool.tile([P, 2, HALF], F32, name="oacc")
+                    oacc = psum.tile([P, 2, HALF], F32, name=f"edge{1 + a}", tag=f"edge{1 + a}")
                     project(oacc[:, 0, :], a)
                     o = keep.tile([P, HALF], F32, name=f"o1{a}")
                     if a == 0:

@@ -1,7 +1,6 @@
 from contextlib import ExitStack
 
 import concourse.mybir as mybir
-from concourse.masks import make_identity
 
 K, T, S, V, H, N = 512, 1024, 512, 256, 512, 256
 FLOPS = 2 * (2 * K * H * S + H * N * V)
@@ -18,8 +17,14 @@ ALU = mybir.AluOpType
 ACT = mybir.ActivationFunctionType
 
 P = 128
-PACK = 4
-HALF = V // 2
+LANES = 4
+GROUP = 16
+QUADRANT = 32
+S_HALF = S // 2
+V_HALF = V // 2
+LOW, HIGH = slice(0, 2), slice(2, 4)
+PRODUCT_BANKS = 5
+OUT_BANKS = 3
 
 
 def tile_picked_edgecv_relu_e_kernel(tc, xT, w1, w2, w3_words, w3_scales, offs, cen, pos1, pos2, pos3, out):
@@ -27,190 +32,160 @@ def tile_picked_edgecv_relu_e_kernel(tc, xT, w1, w2, w3_words, w3_scales, offs, 
     with ExitStack() as ctx:
         lists = ctx.enter_context(tc.tile_pool(name="lists", bufs=1))
         keep = ctx.enter_context(tc.tile_pool(name="keep", bufs=1))
-        psum = ctx.enter_context(tc.psum_pool(name="psum", bufs=1))
+        product_psum = ctx.enter_context(tc.psum_pool(name="product_psum", bufs=PRODUCT_BANKS))
+        out_psum = ctx.enter_context(tc.psum_pool(name="out_psum", bufs=OUT_BANKS))
 
-        def load_list(src, n, name):
-            t = lists.tile([P, n // 16], U16, name=name)
-            nc.sync.dma_start(t[:], src)
-            return t
+        def load_list(src, entries, name):
+            tile = lists.tile([P, entries // GROUP], U16, name=name)
+            nc.sync.dma_start(tile[:], src)
+            return tile
 
-        x_rows = xT.rearrange("(p j) t -> p j t", j=PACK)
-        planes = [keep.tile([P, T], F32, name=f"xplane{j}") for j in range(PACK)]
-        nc.sync.dma_start(planes[0][:], x_rows[:, 0, :])
-        offs_t = load_list(offs, S, "offs_t")
-        for j in range(1, PACK):
-            nc.sync.dma_start(planes[j][:], x_rows[:, j, :])
+        x_rows = xT.rearrange("(p j) c -> p j c", j=LANES)
+        x_lane = [keep.tile([P, T], F32, name=f"x_lane{j}") for j in range(LANES)]
+        nc.sync.dma_start(x_lane[0][:], x_rows[:, 0, :])
+        offs_list = load_list(offs, S, "offs_list")
+        for j in range(1, LANES):
+            nc.sync.dma_start(x_lane[j][:], x_rows[:, j, :])
 
-        def load_w(w, name):
-            t = keep.tile([P, PACK, H], F32, name=f"{name}_raw", tag=f"{name}_raw")
-            nc.sync.dma_start(t[:], w.rearrange("(p j) c -> p j c", j=PACK))
-            return t
+        w2_raw = keep.tile([P, LANES, H], F32, name="w2_raw")
+        for pair in (LOW, HIGH):
+            nc.sync.dma_start(w2_raw[:, pair, :], w2.rearrange("(p j) c -> p j c", j=LANES)[:, pair, :])
+        pos_lists = [load_list(src, V, f"pos_list{d}") for d, src in enumerate((pos1, pos2, pos3))]
+        w1_raw = keep.tile([P, LANES, H], F32, name="w1_raw", tag="w1_raw")
+        nc.sync.dma_start(w1_raw[:], w1.rearrange("(p j) c -> p j c", j=LANES))
+        cen_list = load_list(cen, V, "cen_list")
 
-        w2_raw = keep.tile([P, PACK, H], F32, name="w2_raw")
-        for u in range(2):
-            nc.sync.dma_start(w2_raw[:, 2 * u : 2 * u + 2, :], w2.rearrange("(p j) c -> p j c", j=PACK)[:, 2 * u : 2 * u + 2, :])
-        pos_t = [load_list(src, V, f"pos_t{d}") for d, src in enumerate((pos1, pos2, pos3))]
-        w1_raw = load_w(w1, "w1")
-        cen_t = load_list(cen, V, "cen_t")
-        w3w = keep.tile([P, 2 * N], U8, name="w3w", align_bytes=64)
-        nc.sync.dma_start(w3w[:].bitcast(I32), w3_words[0].bitcast(I32))
-        w3s = keep.tile([P, N], U8, name="w3s", align_bytes=64)
-        nc.vector.memset(w3s[:].bitcast(I32), 0)
-        for q in range(4):
-            nc.sync.dma_start(w3s[32 * q : 32 * q + 4, :].bitcast(I32), w3_scales[0, 4 * q : 4 * q + 4, :].bitcast(I32))
+        w3_codes = keep.tile([P, 2 * N], U8, name="w3_codes", align_bytes=64)
+        nc.sync.dma_start(w3_codes[:].bitcast(I32), w3_words[0].bitcast(I32))
+        w3_scale = keep.tile([P, N], U8, name="w3_scale", align_bytes=64)
+        nc.vector.memset(w3_scale[:].bitcast(I32), 0)
+        for q in range(P // QUADRANT):
+            nc.sync.dma_start(w3_scale[QUADRANT * q : QUADRANT * q + 4, :].bitcast(I32), w3_scales[0, 4 * q : 4 * q + 4, :].bitcast(I32))
 
-        warm = keep.tile([P, 2], F32, name="warm")
-        nc.vector.memset(warm[:, 0:1], 0.0)
-        nc.scalar.activation(warm[:, 1:2], warm[:, 0:1], ACT.Relu)
-
-        ident = keep.tile([P, P], F32, name="ident")
-        make_identity(nc, ident[:])
-
-        SH = S // 2
-        xg = [keep.tile([P, SH, PACK], BF16, name=f"xg{h}", align_bytes=64) for h in range(2)]
-        g01 = keep.tile([P, 2, S], F32, name="g01")
-        g23 = [keep.tile([P, 2, SH], F32, name=f"g23{h}") for h in range(2)]
+        x_bf = [keep.tile([P, S_HALF, LANES], BF16, name=f"x_bf{h}", align_bytes=64) for h in range(2)]
+        picked_low = keep.tile([P, 2, S], F32, name="picked_low")
+        picked_high = [keep.tile([P, 2, S_HALF], F32, name=f"picked_high{h}") for h in range(2)]
         for j in range(2):
-            nc.vector.tensor_copy(g01[:, j, :], planes[j][:].indirect(offs_t[:]))
+            nc.vector.tensor_copy(picked_low[:, j, :], x_lane[j][:].indirect(offs_list[:]))
         for h in range(2):
-            nc.scalar.copy(xg[h][:, :, 0:2], g01[:, :, h * SH : (h + 1) * SH].rearrange("p j s -> p s j"))
+            nc.scalar.copy(x_bf[h][:, :, LOW], picked_low[:, :, h * S_HALF : (h + 1) * S_HALF].rearrange("p j s -> p s j"))
+        half_columns = S_HALF // GROUP
         for j in range(2):
             for h in range(2):
-                nc.vector.tensor_copy(g23[h][:, j, :], planes[2 + j][:].indirect(offs_t[:, h * 16 : (h + 1) * 16]))
-        nc.scalar.copy(xg[0][:, :, 2:4], g23[0][:].rearrange("p j s -> p s j"))
-        nc.vector.tensor_copy(xg[1][:, :, 2:4], g23[1][:].rearrange("p j s -> p s j"))
-        xq = keep.tile([P, S], U32, name="xq", align_bytes=64)
-        xs = keep.tile([P, S], U8, name="xs", align_bytes=64)
+                entries = offs_list[:, h * half_columns : (h + 1) * half_columns]
+                nc.vector.tensor_copy(picked_high[h][:, j, :], x_lane[2 + j][:].indirect(entries))
+        nc.scalar.copy(x_bf[0][:, :, HIGH], picked_high[0][:].rearrange("p j s -> p s j"))
+        nc.vector.tensor_copy(x_bf[1][:, :, HIGH], picked_high[1][:].rearrange("p j s -> p s j"))
+        x_codes = keep.tile([P, S], U32, name="x_codes", align_bytes=64)
+        x_scale = keep.tile([P, S], U8, name="x_scale", align_bytes=64)
         for h in range(2):
-            cols = slice(h * SH, (h + 1) * SH)
-            nc.vector.quantize_mx(out=xq[:, cols].bitcast(FP8X4), scales=xs[:, cols], in_=xg[h][:].rearrange("p s j -> p (s j)"))
+            cols = slice(h * S_HALF, (h + 1) * S_HALF)
+            nc.vector.quantize_mx(out=x_codes[:, cols].bitcast(FP8X4), scales=x_scale[:, cols], in_=x_bf[h][:].rearrange("p s j -> p (s j)"))
 
-        def cast(engine_copy, raw, ts, name):
-            n = ts.stop - ts.start
-            wg = keep.tile([P, n, P, PACK], BF16, name=f"{name}_g{ts.start}", align_bytes=64)
-            engine_copy(
-                wg[:].rearrange("p t m j -> p m t j"),
-                raw[:].rearrange("p j (m t) -> p m t j", t=PACK)[:, :, ts, :],
-            )
-            return wg
+        def dealt(raw):
+            return raw[:].rearrange("p j (m t) -> p m t j", t=LANES)
 
-        def quantise(wg, n, name):
-            wq = keep.tile([P, n * P], U32, name=f"{name}_q", align_bytes=64)
-            ws = keep.tile([P, n * P], U8, name=f"{name}_s", align_bytes=64)
-            nc.vector.quantize_mx(out=wq[:].bitcast(FP8X4), scales=ws[:], in_=wg[:].rearrange("p t m j -> p (t m j)"))
-            return [(wq[:, i * P : (i + 1) * P], ws[:, i * P : (i + 1) * P]) for i in range(n)]
+        def deal(engine_copy, raw, lanes, tag):
+            w_bf = keep.tile([P, lanes.stop - lanes.start, P, LANES], BF16, name=tag, tag=tag, align_bytes=64)
+            engine_copy(w_bf[:].rearrange("p t m j -> p m t j"), dealt(raw)[:, :, lanes, :])
+            return w_bf
 
-        def product(op, r, banks):
-            width = S // len(banks)
-            for i, bank in enumerate(banks):
+        def quantise(w_bf, name):
+            count = w_bf.shape[1]
+            codes = keep.tile([P, count * P], U32, name=f"{name}_codes", align_bytes=64)
+            scale = keep.tile([P, count * P], U8, name=f"{name}_scale", align_bytes=64)
+            nc.vector.quantize_mx(out=codes[:].bitcast(FP8X4), scales=scale[:], in_=w_bf[:].rearrange("p t m j -> p (t m j)"))
+            return [(codes[:, i * P : (i + 1) * P], scale[:, i * P : (i + 1) * P]) for i in range(count)]
+
+        def product(weights, tag, name, pieces=1):
+            rows = keep.tile([P, S], F32, name=name, tag=tag)
+            width = S // pieces
+            for i in range(pieces):
                 cols = slice(i * width, (i + 1) * width)
-                acc = psum.tile([P, S], F32, name=bank, tag=bank)
-                nc.tensor.matmul_mx(out=acc[:, 0:width], lhsT=op[0].bitcast(FP8X4), lhsT_scale=op[1], rhs=xq[:, cols].bitcast(FP8X4), rhs_scale=xs[:, cols], start=True, stop=True)
-                nc.scalar.copy(r[:, cols], acc[:, 0:width])
-            return r
-
-        def row_tile(name, tag=None):
-            return keep.tile([P, S], F32, name=name, tag=tag or name)[:]
-
-        wg0 = keep.tile([P, 1, P, PACK], BF16, name="w2_one", tag="w2_one", align_bytes=64)
-        w2_dealt = w2_raw[:].rearrange("p j (m t) -> p m t j", t=PACK)
-        for u in range(2):
-            nc.scalar.copy(wg0[:, 0, :, 2 * u : 2 * u + 2], w2_dealt[:, :, 0, 2 * u : 2 * u + 2])
-        ops = quantise(wg0, 1, "w2a")
-        wg1 = cast(nc.scalar.copy, w2_raw, slice(1, 2), "w2")
-        wg23 = keep.tile([P, 2, P, PACK], BF16, name="w2_one", tag="w2_one", align_bytes=64)
-        nc.vector.tensor_copy(wg23[:].rearrange("p t m j -> p m t j"), w2_dealt[:, :, 2:4, :])
-        e = [product(ops[0], row_tile("e0"), ["a0", "a1"])]
-        ops = quantise(wg1, 1, "w2b") + quantise(wg23, 2, "w2c")
-        g = [keep.tile([P, PACK, V], F32, name=f"g{d}") for d in range(3)]
-        e.append(product(ops[0], row_tile("e1"), ["a2"]))
-        w1g = cast(nc.scalar.copy, w1_raw, slice(0, 4), "w1")
-        w1ops = quantise(w1g, 4, "w1")
-        e.append(product(ops[1], row_tile("e2", "w1_raw"), ["a3"]))
-        y = [product(w1ops[t], row_tile(f"y{t}"), [f"a{t}"]) for t in range(2)]
-        e.append(product(ops[2], row_tile("e3"), ["a0"]))
-        y.append(product(w1ops[2], row_tile("y2"), ["a1"]))
-        edge = [psum.tile([P, 2, 2, P], F32, name=f"edge{d}", tag=f"edge{d}") for d in range(3)]
-
-        def turn(d, t, src, first, last):
-            for h in range(2):
-                nc.tensor.matmul(edge[d][:, t, h, :], lhsT=src[:, t, h * HALF : (h + 1) * HALF], rhs=ident[:], is_transpose=True, start=first and h == 0, stop=last and h == 1)
-
-        def fetch(t):
-            for d in range(3):
-                nc.vector.tensor_copy(g[d][:, t, :], e[t].indirect(pos_t[d][:]))
-
-        for t in range(3):
-            fetch(t)
-        for t in range(2):
-            for d in range(3):
-                turn(d, t, g[d], t == 0, False)
-        yc = keep.tile([P, 2, V], F32, name="yc")
-        for t in range(2):
-            nc.vector.tensor_copy(yc[:, t, :], y[t].indirect(cen_t[:]))
-        r = []
-        for d in range(3):
-            for t in range(2):
-                turn(d, t, yc, False, t == 1)
-            rd = keep.tile([P, 4 * P], BF16, name=f"r{d}", tag=f"r{d}")
-            nc.scalar.activation(rd[:].rearrange("v (h p t) -> v h p t", h=2, t=2), edge[d][:].rearrange("v t h p -> v h p t"), ACT.Relu)
-            r.append(rd)
-        y.append(product(w1ops[3], row_tile("y3"), ["edge0"]))
-        fetch(3)
-        m12 = keep.tile([P, 2, V], F32, name="m12")
-        nc.vector.tensor_tensor(m12[:], g[0][:, 2:4, :], g[1][:, 2:4, :], ALU.max)
-        r12 = keep.tile([P, 4 * P], BF16, name="r12", tag="r12")
-        nc.vector.tensor_tensor(r12[:], r[0][:], r[1][:], ALU.max)
-        m = keep.tile([P, 2, V], F32, name="m", tag="r0")
-        nc.vector.tensor_tensor(m[:], m12[:], g[2][:, 2:4, :], ALU.max)
-        zt = keep.tile([P, 4 * P], BF16, name="zt")
-        nc.vector.tensor_tensor(zt[:], r12[:], r[2][:], ALU.max)
-        zs_in = [keep.tile([P, HALF, PACK], BF16, name=f"z{h}", align_bytes=64) for h in range(2)]
-        for h in range(2):
-            back = psum.tile([P, HALF], F32, name=f"a{h}", tag=f"a{h}")
-            nc.tensor.transpose(back[:], zt[:, 2 * P * h : 2 * P * (h + 1)].bitcast(F32), ident[:])
-            nc.scalar.copy(zs_in[h][:, :, 0:2], back[:].bitcast(BF16).rearrange("p (v t) -> p v t", t=2))
-
-        out_v = out.rearrange("(a p) v -> p a v", p=P)
-        for h in range(2):
-            cols = slice(h * HALF, (h + 1) * HALF)
-            s = keep.tile([P, 2, HALF], F32, name=f"s{h}", tag=("r2", "r12")[h])
-            for t in range(2):
-                nc.vector.tensor_tensor(s[:, t, :], y[2 + t].indirect(cen_t[:, h * 8 : (h + 1) * 8]), m[:, t, cols], ALU.add)
-            z = zs_in[h]
-            if h == 0:
-                nc.scalar.activation(z[:, :, 2:4], s[:].rearrange("p t v -> p v t"), ACT.Relu)
-            else:
-                nc.vector.tensor_scalar(z[:, :, 2:4], s[:].rearrange("p t v -> p v t"), 0.0, None, ALU.max)
-            zq = keep.tile([P, HALF], U32, name=f"zq{h}", align_bytes=64)
-            zs = keep.tile([P, HALF], U8, name=f"zs{h}", align_bytes=64)
-            nc.vector.quantize_mx(out=zq[:].bitcast(FP8X4), scales=zs[:], in_=z[:].rearrange("p v t -> p (v t)"))
-            def project(dst, a):
+                bank = product_psum.tile([P, S], F32, name="bank")
                 nc.tensor.matmul_mx(
-                    out=dst,
-                    lhsT=w3w[:, 2 * P * a : 2 * P * (a + 1)].bitcast(FP4X4),
-                    lhsT_scale=w3s[:, P * a : P * (a + 1)],
-                    rhs=zq[:].bitcast(FP8X4),
-                    rhs_scale=zs[:],
+                    out=bank[:, 0:width],
+                    lhsT=weights[0].bitcast(FP8X4),
+                    lhsT_scale=weights[1],
+                    rhs=x_codes[:, cols].bitcast(FP8X4),
+                    rhs_scale=x_scale[:, cols],
                     start=True,
                     stop=True,
                 )
+                nc.scalar.copy(rows[:, cols], bank[:, 0:width])
+            return rows
 
-            if h == 0:
-                oacc = psum.tile([P, 2, HALF], F32, name="a2", tag="a2")
-                for a in range(2):
-                    project(oacc[:, a, :], a)
-                o = keep.tile([P, 2, HALF], F32, name="o0")
-                nc.scalar.copy(o[:], oacc[:])
-                nc.sync.dma_start(out_v[:, :, cols], o[:])
-            else:
-                for a in range(2):
-                    oacc = psum.tile([P, 2, HALF], F32, name=f"edge{1 + a}", tag=f"edge{1 + a}")
-                    project(oacc[:, 0, :], a)
-                    o = keep.tile([P, HALF], F32, name=f"o1{a}")
-                    if a == 0:
-                        nc.vector.tensor_copy(o[:], oacc[:, 0, :])
-                        nc.sync.dma_start(out_v[:, a, cols], o[:])
-                    else:
-                        nc.scalar.copy(o[:], oacc[:, 0, :])
-                        nc.scalar.dma_start(out_v[:, a, cols], o[:])
+        w2_bf0 = keep.tile([P, 1, P, LANES], BF16, name="w2_first", tag="w2_first", align_bytes=64)
+        for pair in (LOW, HIGH):
+            nc.scalar.copy(w2_bf0[:, 0, :, pair], dealt(w2_raw)[:, :, 0, pair])
+        w2_ops = quantise(w2_bf0, "w2_lane0")
+        w2_bf1 = deal(nc.scalar.copy, w2_raw, slice(1, 2), "w2_second")
+        w2_bf23 = deal(nc.vector.tensor_copy, w2_raw, HIGH, "w2_first")
+        e = [product(w2_ops[0], "e0", "e0", pieces=2)]
+        w2_ops = w2_ops + quantise(w2_bf1, "w2_lane1") + quantise(w2_bf23, "w2_lanes23")
+        neighbour = [keep.tile([P, LANES, V], F32, name=f"neighbour{d}") for d in range(3)]
+        largest_of_two = keep.tile([P, LANES, V], F32, name="largest_of_two")
+        largest = keep.tile([P, LANES, V], F32, name="largest")
+        e.append(product(w2_ops[1], "e1", "e1"))
+        w1_ops = quantise(deal(nc.scalar.copy, w1_raw, slice(0, LANES), "w1_bf"), "w1")
+        e.append(product(w2_ops[2], "w1_raw", "e2"))
+        e.append(product(w2_ops[3], "e3", "e3"))
+        y = [product(w1_ops[t], f"y{t}", f"y{t}") for t in range(LANES)]
+
+        for t in range(LANES):
+            for d in range(3):
+                nc.vector.tensor_copy(neighbour[d][:, t, :], e[t][:].indirect(pos_lists[d][:]))
+        for pair in (LOW, HIGH):
+            nc.vector.tensor_tensor(largest_of_two[:, pair, :], neighbour[0][:, pair, :], neighbour[1][:, pair, :], ALU.max)
+        for pair in (LOW, HIGH):
+            nc.vector.tensor_tensor(largest[:, pair, :], largest_of_two[:, pair, :], neighbour[2][:, pair, :], ALU.max)
+
+        out_rows = out.rearrange("(a p) v -> p a v", p=P)
+        centre_columns = V_HALF // GROUP
+
+        def edge_sums(h):
+            sums = keep.tile([P, LANES, V_HALF], F32, name=f"sums{h}")
+            entries = cen_list[:, h * centre_columns : (h + 1) * centre_columns]
+            for t in range(LANES):
+                nc.vector.tensor_tensor(sums[:, t, :], y[t][:].indirect(entries), largest[:, t, h * V_HALF : (h + 1) * V_HALF], ALU.add)
+            return sums[:].rearrange("p t v -> p v t")
+
+        def quantise_z(z_bf, h):
+            codes = keep.tile([P, V_HALF], U32, name=f"z_codes{h}", align_bytes=64)
+            scale = keep.tile([P, V_HALF], U8, name=f"z_scale{h}", align_bytes=64)
+            nc.vector.quantize_mx(out=codes[:].bitcast(FP8X4), scales=scale[:], in_=z_bf[:].rearrange("p v t -> p (v t)"))
+            return codes, scale
+
+        def project(dst, a, z_op):
+            nc.tensor.matmul_mx(
+                out=dst,
+                lhsT=w3_codes[:, 2 * P * a : 2 * P * (a + 1)].bitcast(FP4X4),
+                lhsT_scale=w3_scale[:, P * a : P * (a + 1)],
+                rhs=z_op[0][:].bitcast(FP8X4),
+                rhs_scale=z_op[1][:],
+                start=True,
+                stop=True,
+            )
+
+        sums = edge_sums(0)
+        z_bf = keep.tile([P, V_HALF, LANES], BF16, name="z_bf0", align_bytes=64)
+        nc.scalar.activation(z_bf[:], sums, ACT.Relu)
+        z_op = quantise_z(z_bf, 0)
+        out_bank = out_psum.tile([P, 2, V_HALF], F32, name="out_bank")
+        for a in range(2):
+            project(out_bank[:, a, :], a, z_op)
+        staged = keep.tile([P, 2, V_HALF], F32, name="staged_first")
+        nc.scalar.copy(staged[:], out_bank[:])
+        nc.sync.dma_start(out_rows[:, :, 0:V_HALF], staged[:])
+
+        sums = edge_sums(1)
+        z_bf = keep.tile([P, V_HALF, LANES], BF16, name="z_bf1", align_bytes=64)
+        nc.scalar.activation(z_bf[:, :, LOW], sums[:, :, LOW], ACT.Relu)
+        nc.vector.tensor_scalar(z_bf[:, :, HIGH], sums[:, :, HIGH], 0.0, None, ALU.max)
+        z_op = quantise_z(z_bf, 1)
+        for a, (engine_copy, queue) in enumerate(((nc.vector.tensor_copy, nc.sync), (nc.scalar.copy, nc.scalar))):
+            out_bank = out_psum.tile([P, 2, V_HALF], F32, name="out_bank")
+            project(out_bank[:, 0, :], a, z_op)
+            staged = keep.tile([P, V_HALF], F32, name=f"staged_second{a}")
+            engine_copy(staged[:], out_bank[:, 0, :])
+            queue.dma_start(out_rows[:, a, V_HALF:V], staged[:])

@@ -47,13 +47,13 @@ def tile_picked_edgecv_relu_e_kernel(tc, xT, w1, w2, w3_words, w3_scales, offs, 
         for j in range(1, LANES):
             nc.sync.dma_start(x_lane[j][:], x_rows[:, j, :])
 
-        w2_raw = keep.tile([P, LANES, H], F32, name="w2_raw")
+        w1_raw = keep.tile([P, LANES, H], F32, name="w1_raw")
         for pair in (LOW, HIGH):
-            nc.sync.dma_start(w2_raw[:, pair, :], w2.rearrange("(p j) c -> p j c", j=LANES)[:, pair, :])
-        pos_lists = [load_list(src, V, f"pos_list{d}") for d, src in enumerate((pos1, pos2, pos3))]
-        w1_raw = keep.tile([P, LANES, H], F32, name="w1_raw", tag="w1_raw")
-        nc.sync.dma_start(w1_raw[:], w1.rearrange("(p j) c -> p j c", j=LANES))
+            nc.sync.dma_start(w1_raw[:, pair, :], w1.rearrange("(p j) c -> p j c", j=LANES)[:, pair, :])
         cen_list = load_list(cen, V, "cen_list")
+        w2_raw = keep.tile([P, LANES, H], F32, name="w2_raw")
+        nc.sync.dma_start(w2_raw[:], w2.rearrange("(p j) c -> p j c", j=LANES))
+        pos_lists = [load_list(src, V, f"pos_list{d}") for d, src in enumerate((pos1, pos2, pos3))]
 
         w3_codes = keep.tile([P, 2 * N], U8, name="w3_codes", align_bytes=64)
         nc.sync.dma_start(w3_codes[:].bitcast(I32), w3_words[0].bitcast(I32))
@@ -115,45 +115,53 @@ def tile_picked_edgecv_relu_e_kernel(tc, xT, w1, w2, w3_words, w3_scales, offs, 
                 nc.scalar.copy(rows[:, cols], bank[:, 0:width])
             return rows
 
-        w2_bf0 = keep.tile([P, 1, P, LANES], BF16, name="w2_first", tag="w2_first", align_bytes=64)
+        w1_bf0 = keep.tile([P, 1, P, LANES], BF16, name="w1_first", tag="w1_first", align_bytes=64)
         for pair in (LOW, HIGH):
-            nc.scalar.copy(w2_bf0[:, 0, :, pair], dealt(w2_raw)[:, :, 0, pair])
-        w2_ops = quantise(w2_bf0, "w2_lane0")
-        w2_bf1 = deal(nc.scalar.copy, w2_raw, slice(1, 2), "w2_second")
-        w2_bf23 = deal(nc.vector.tensor_copy, w2_raw, HIGH, "w2_first")
-        e = [product(w2_ops[0], "e0", "e0", pieces=2)]
-        w2_ops = w2_ops + quantise(w2_bf1, "w2_lane1") + quantise(w2_bf23, "w2_lanes23")
-        neighbour = [keep.tile([P, LANES, V], F32, name=f"neighbour{d}") for d in range(3)]
-        largest_of_two = keep.tile([P, LANES, V], F32, name="largest_of_two")
-        largest = keep.tile([P, LANES, V], F32, name="largest")
-        e.append(product(w2_ops[1], "e1", "e1"))
-        w1_ops = quantise(deal(nc.scalar.copy, w1_raw, slice(0, LANES), "w1_bf"), "w1")
-        e.append(product(w2_ops[2], "w1_raw", "e2"))
-        e.append(product(w2_ops[3], "e3", "e3"))
-        y = [product(w1_ops[t], f"y{t}", f"y{t}") for t in range(LANES)]
-
+            nc.scalar.copy(w1_bf0[:, 0, :, pair], dealt(w1_raw)[:, :, 0, pair])
+        w1_ops = quantise(w1_bf0, "w1_lane0")
+        w1_bf1 = deal(nc.scalar.copy, w1_raw, slice(1, 2), "w1_second")
+        w1_bf23 = deal(nc.vector.tensor_copy, w1_raw, HIGH, "w1_first")
+        y = [product(w1_ops[0], "y0", "y0", pieces=2)]
+        w1_ops = w1_ops + quantise(w1_bf1, "w1_lane1") + quantise(w1_bf23, "w1_lanes23")
+        y.extend([product(w1_ops[t], f"y{t}", f"y{t}") for t in range(1, LANES)])
+        w2_low = quantise(deal(nc.vector.tensor_copy, w2_raw, LOW, "w2_low"), "w2_low")
+        centre = keep.tile([P, LANES, V], F32, name="centre", tag="w2_low", align_bytes=64)
         for t in range(LANES):
+            nc.vector.tensor_copy(centre[:, t, :], y[t][:].indirect(cen_list[:]))
+        e = [product(w2_low[0], "e0", "e0")]
+        w2_high = quantise(deal(nc.scalar.copy, w2_raw, HIGH, "w2_high"), "w2_high")
+        e.append(product(w2_low[1], "e1", "e1"))
+        e.extend([product(w2_high[i], f"e{2 + i}", f"e{2 + i}") for i in range(2)])
+
+        edge_bf = [keep.tile([P, V, LANES], BF16, name=f"edge_bf{d}") for d in range(3)]
+        for u, pair in enumerate((LOW, HIGH)):
             for d in range(3):
-                nc.vector.tensor_copy(neighbour[d][:, t, :], e[t][:].indirect(pos_lists[d][:]))
-        for pair in (LOW, HIGH):
-            nc.vector.tensor_tensor(largest_of_two[:, pair, :], neighbour[0][:, pair, :], neighbour[1][:, pair, :], ALU.max)
-        for pair in (LOW, HIGH):
-            nc.vector.tensor_tensor(largest[:, pair, :], largest_of_two[:, pair, :], neighbour[2][:, pair, :], ALU.max)
+                edge = keep.tile([P, 2, V], F32, name=f"edge{u}{d}", tag=f"edge{(3 * u + d) % 4}")
+                pieces = 2 if (u, d) == (1, 2) else 1
+                width = V // pieces
+                for h in range(pieces):
+                    cols = slice(h * width, (h + 1) * width)
+                    entries = pos_lists[d][:, h * width // GROUP : (h + 1) * width // GROUP]
+                    for i in range(2):
+                        nc.vector.tensor_tensor(edge[:, i, cols], e[2 * u + i][:].indirect(entries), centre[:, 2 * u + i, cols], ALU.add)
+                    nc.scalar.activation(edge_bf[d][:, cols, pair], edge[:, :, cols].rearrange("p t v -> p v t"), ACT.Relu)
 
         out_rows = out.rearrange("(a p) v -> p a v", p=P)
-        centre_columns = V_HALF // GROUP
 
-        def edge_sums(h):
-            sums = keep.tile([P, LANES, V_HALF], F32, name=f"sums{h}")
-            entries = cen_list[:, h * centre_columns : (h + 1) * centre_columns]
-            for t in range(LANES):
-                nc.vector.tensor_tensor(sums[:, t, :], y[t][:].indirect(entries), largest[:, t, h * V_HALF : (h + 1) * V_HALF], ALU.add)
-            return sums[:].rearrange("p t v -> p v t")
+        def flat(tile, h):
+            return tile[:, h * V_HALF : (h + 1) * V_HALF, :].rearrange("p v t -> p (v t)")
 
-        def quantise_z(z_bf, h):
+        larger = keep.tile([P, V, LANES], BF16, name="larger")
+        z_all = keep.tile([P, V, LANES], BF16, name="z_all", align_bytes=64)
+        for h in range(2):
+            nc.vector.tensor_tensor(flat(larger, h), flat(edge_bf[0], h), flat(edge_bf[1], h), ALU.max)
+        for h in range(2):
+            nc.vector.tensor_tensor(flat(z_all, h), flat(larger, h), flat(edge_bf[2], h), ALU.max)
+
+        def quantise_z(h):
             codes = keep.tile([P, V_HALF], U32, name=f"z_codes{h}", align_bytes=64)
             scale = keep.tile([P, V_HALF], U8, name=f"z_scale{h}", align_bytes=64)
-            nc.vector.quantize_mx(out=codes[:].bitcast(FP8X4), scales=scale[:], in_=z_bf[:].rearrange("p v t -> p (v t)"))
+            nc.vector.quantize_mx(out=codes[:].bitcast(FP8X4), scales=scale[:], in_=flat(z_all, h))
             return codes, scale
 
         def project(dst, a, z_op):
@@ -167,10 +175,7 @@ def tile_picked_edgecv_relu_e_kernel(tc, xT, w1, w2, w3_words, w3_scales, offs, 
                 stop=True,
             )
 
-        sums = edge_sums(0)
-        z_bf = keep.tile([P, V_HALF, LANES], BF16, name="z_bf0", align_bytes=64)
-        nc.scalar.activation(z_bf[:], sums, ACT.Relu)
-        z_op = quantise_z(z_bf, 0)
+        z_op = quantise_z(0)
         out_bank = out_psum.tile([P, 2, V_HALF], F32, name="out_bank")
         for a in range(2):
             project(out_bank[:, a, :], a, z_op)
@@ -178,11 +183,7 @@ def tile_picked_edgecv_relu_e_kernel(tc, xT, w1, w2, w3_words, w3_scales, offs, 
         nc.scalar.copy(staged[:], out_bank[:])
         nc.sync.dma_start(out_rows[:, :, 0:V_HALF], staged[:])
 
-        sums = edge_sums(1)
-        z_bf = keep.tile([P, V_HALF, LANES], BF16, name="z_bf1", align_bytes=64)
-        nc.scalar.activation(z_bf[:, :, LOW], sums[:, :, LOW], ACT.Relu)
-        nc.vector.tensor_scalar(z_bf[:, :, HIGH], sums[:, :, HIGH], 0.0, None, ALU.max)
-        z_op = quantise_z(z_bf, 1)
+        z_op = quantise_z(1)
         for a, (engine_copy, queue) in enumerate(((nc.vector.tensor_copy, nc.sync), (nc.scalar.copy, nc.scalar))):
             out_bank = out_psum.tile([P, 2, V_HALF], F32, name="out_bank")
             project(out_bank[:, 0, :], a, z_op)

@@ -133,8 +133,9 @@ def tile_picked_edgecv_relu_e_kernel(tc, xT, w1, w2, w3_words, w3_scales, offs, 
         e.append(product(w2_low[1], "e1", "e1"))
         e.extend([product(w2_high[i], f"e{2 + i}", f"e{2 + i}") for i in range(2)])
 
-        edge_bf = [keep.tile([P, V, LANES], BF16, name=f"edge_bf{d}") for d in range(3)]
-        for u, pair in enumerate((LOW, HIGH)):
+        edge_bf = [keep.tile([P, 2, V, 2], BF16, name=f"edge_bf{d}") for d in range(3)]
+        larger = keep.tile([P, 2, V, 2], BF16, name="larger")
+        for u in range(2):
             for d in range(3):
                 edge = keep.tile([P, 2, V], F32, name=f"edge{u}{d}", tag=f"edge{(3 * u + d) % 4}")
                 pieces = 2 if (u, d) == (1, 2) else 1
@@ -144,19 +145,21 @@ def tile_picked_edgecv_relu_e_kernel(tc, xT, w1, w2, w3_words, w3_scales, offs, 
                     entries = pos_lists[d][:, h * width // GROUP : (h + 1) * width // GROUP]
                     for i in range(2):
                         nc.vector.tensor_tensor(edge[:, i, cols], e[2 * u + i][:].indirect(entries), centre[:, 2 * u + i, cols], ALU.add)
-                    nc.scalar.activation(edge_bf[d][:, cols, pair], edge[:, :, cols].rearrange("p t v -> p v t"), ACT.Relu)
+                    nc.scalar.activation(edge_bf[d][:, u, cols, :], edge[:, :, cols].rearrange("p t v -> p v t"), ACT.Relu)
 
         out_rows = out.rearrange("(a p) v -> p a v", p=P)
 
         def flat(tile, h):
             return tile[:, h * V_HALF : (h + 1) * V_HALF, :].rearrange("p v t -> p (v t)")
 
-        larger = keep.tile([P, V, LANES], BF16, name="larger")
         z_all = keep.tile([P, V, LANES], BF16, name="z_all", align_bytes=64)
         for h in range(2):
-            nc.vector.tensor_tensor(flat(larger, h), flat(edge_bf[0], h), flat(edge_bf[1], h), ALU.max)
+            cols = slice(h * V_HALF, (h + 1) * V_HALF)
+            nc.vector.tensor_tensor(larger[:, :, cols, :], edge_bf[0][:, :, cols, :], edge_bf[1][:, :, cols, :], ALU.max)
         for h in range(2):
-            nc.vector.tensor_tensor(flat(z_all, h), flat(larger, h), flat(edge_bf[2], h), ALU.max)
+            cols = slice(h * V_HALF, (h + 1) * V_HALF)
+            woven = [tile[:, :, cols, :].rearrange("p u v t -> p v u t") for tile in (larger, edge_bf[2])]
+            nc.vector.tensor_tensor(z_all[:, cols, :].rearrange("p v (u t) -> p v u t", u=2), woven[0], woven[1], ALU.max)
 
         def quantise_z(h):
             codes = keep.tile([P, V_HALF], U32, name=f"z_codes{h}", align_bytes=64)

@@ -51,8 +51,9 @@ def tile_picked_edgecv_relu_e_kernel(tc, xT, w1, w2, w3_words, w3_scales, offs, 
         for pair in (LOW, HIGH):
             nc.sync.dma_start(w1_raw[:, pair, :], w1.rearrange("(p j) c -> p j c", j=LANES)[:, pair, :])
         cen_list = load_list(cen, V, "cen_list")
-        w2_raw = keep.tile([P, LANES, H], F32, name="w2_raw")
-        nc.sync.dma_start(w2_raw[:], w2.rearrange("(p j) c -> p j c", j=LANES))
+        w2_raw = [keep.tile([P, LANES, H // 2], F32, name=f"w2_raw{side}", tag=f"w2_raw{side}") for side in range(2)]
+        for side in range(2):
+            nc.sync.dma_start(w2_raw[side][:], w2.rearrange("(p j) (s c) -> p s j c", j=LANES, s=2)[:, side])
         pos_lists = [load_list(src, V, f"pos_list{d}") for d, src in enumerate((pos1, pos2, pos3))]
 
         w3_codes = keep.tile([P, 2 * N], U8, name="w3_codes", align_bytes=64)
@@ -97,8 +98,7 @@ def tile_picked_edgecv_relu_e_kernel(tc, xT, w1, w2, w3_words, w3_scales, offs, 
             nc.vector.quantize_mx(out=codes[:].bitcast(FP8X4), scales=scale[:], in_=w_bf[:].rearrange("p t m j -> p (t m j)"))
             return [(codes[:, i * P : (i + 1) * P], scale[:, i * P : (i + 1) * P]) for i in range(count)]
 
-        def product(weights, tag, name, pieces=1):
-            rows = keep.tile([P, S], F32, name=name, tag=tag)
+        def product(weights, rows, pieces=1):
             width = S // pieces
             for i in range(pieces):
                 cols = slice(i * width, (i + 1) * width)
@@ -121,17 +121,18 @@ def tile_picked_edgecv_relu_e_kernel(tc, xT, w1, w2, w3_words, w3_scales, offs, 
         w1_ops = quantise(w1_bf0, "w1_lane0")
         w1_bf1 = deal(nc.scalar.copy, w1_raw, slice(1, 2), "w1_second")
         w1_bf23 = deal(nc.vector.tensor_copy, w1_raw, HIGH, "w1_first")
-        y = [product(w1_ops[0], "y0", "y0", pieces=2)]
+        y = [product(w1_ops[0], keep.tile([P, S], F32, name="y0"), pieces=2)]
         w1_ops = w1_ops + quantise(w1_bf1, "w1_lane1") + quantise(w1_bf23, "w1_lanes23")
-        y.extend([product(w1_ops[t], f"y{t}", f"y{t}") for t in range(1, LANES)])
-        w2_low = quantise(deal(nc.vector.tensor_copy, w2_raw, LOW, "w2_low"), "w2_low")
-        centre = keep.tile([P, LANES, V], F32, name="centre", tag="w2_low", align_bytes=64)
+        w2_bf = keep.tile([P, LANES, P, LANES], BF16, name="w2_bf", align_bytes=64)
+        for side, engine_copy in enumerate((nc.vector.tensor_copy, nc.scalar.copy)):
+            engine_copy(w2_bf[:, :, side * P // 2 : (side + 1) * P // 2, :].rearrange("p t m j -> p m t j"), dealt(w2_raw[side]))
+        y_rest = keep.tile([P, 3 * S], F32, name="y_rest", tag="w2_raw1")
+        y.extend([product(w1_ops[t], y_rest[:, (t - 1) * S : t * S]) for t in range(1, LANES)])
+        w2_ops = quantise(w2_bf, "w2")
+        centre = keep.tile([P, LANES, V], F32, name="centre", tag="w2_raw0")
         for t in range(LANES):
             nc.vector.tensor_copy(centre[:, t, :], y[t][:].indirect(cen_list[:]))
-        e = [product(w2_low[0], "e0", "e0")]
-        w2_high = quantise(deal(nc.scalar.copy, w2_raw, HIGH, "w2_high"), "w2_high")
-        e.append(product(w2_low[1], "e1", "e1"))
-        e.extend([product(w2_high[i], f"e{2 + i}", f"e{2 + i}") for i in range(2)])
+        e = [product(w2_ops[t], keep.tile([P, S], F32, name=f"e{t}")) for t in range(LANES)]
 
         edge_bf = [keep.tile([P, 2, V, 2], BF16, name=f"edge_bf{d}") for d in range(3)]
         larger = keep.tile([P, 2, V, 2], BF16, name="larger")

@@ -23,6 +23,7 @@ QUADRANT = 32
 S_HALF = S // 2
 V_HALF = V // 2
 LOW, HIGH = slice(0, 2), slice(2, 4)
+SCALAR_PLACES = 80
 PRODUCT_BANKS = 5
 OUT_BANKS = 3
 
@@ -50,10 +51,10 @@ def tile_picked_edgecv_relu_e_kernel(tc, xT, w1, w2, w3_words, w3_scales, offs, 
         w1_raw = keep.tile([P, LANES, H], F32, name="w1_raw")
         for pair in (LOW, HIGH):
             nc.sync.dma_start(w1_raw[:, pair, :], w1.rearrange("(p j) c -> p j c", j=LANES)[:, pair, :])
-        cen_list = load_list(cen, V, "cen_list")
         w2_raw = [keep.tile([P, LANES, H // 2], F32, name=f"w2_raw{side}", tag=f"w2_raw{side}") for side in range(2)]
         for side in range(2):
             nc.sync.dma_start(w2_raw[side][:], w2.rearrange("(p j) (s c) -> p s j c", j=LANES, s=2)[:, side])
+        cen_list = load_list(cen, V, "cen_list")
         pos_lists = [load_list(src, V, f"pos_list{d}") for d, src in enumerate((pos1, pos2, pos3))]
 
         w3_codes = keep.tile([P, 2 * N], U8, name="w3_codes", align_bytes=64)
@@ -115,23 +116,20 @@ def tile_picked_edgecv_relu_e_kernel(tc, xT, w1, w2, w3_words, w3_scales, offs, 
                 nc.scalar.copy(rows[:, cols], bank[:, 0:width])
             return rows
 
-        w1_bf0 = keep.tile([P, 1, P, LANES], BF16, name="w1_first", tag="w1_first", align_bytes=64)
-        for pair in (LOW, HIGH):
-            nc.scalar.copy(w1_bf0[:, 0, :, pair], dealt(w1_raw)[:, :, 0, pair])
-        w1_ops = quantise(w1_bf0, "w1_lane0")
-        w1_bf1 = deal(nc.scalar.copy, w1_raw, slice(1, 2), "w1_second")
-        w1_bf23 = deal(nc.vector.tensor_copy, w1_raw, HIGH, "w1_first")
-        y = [product(w1_ops[0], keep.tile([P, S], F32, name="y0"), pieces=2)]
-        w1_ops = w1_ops + quantise(w1_bf1, "w1_lane1") + quantise(w1_bf23, "w1_lanes23")
+        w1_bf = keep.tile([P, LANES, P, LANES], BF16, name="w1_bf", align_bytes=64)
+        for places, engine_copy in ((slice(0, SCALAR_PLACES), nc.scalar.copy), (slice(SCALAR_PLACES, P), nc.vector.tensor_copy)):
+            engine_copy(w1_bf[:, :, places, :].rearrange("p t m j -> p m t j"), dealt(w1_raw)[:, places])
+        w1_ops = quantise(w1_bf[:, LOW], "w1_low") + quantise(w1_bf[:, HIGH], "w1_high")
         w2_bf = keep.tile([P, LANES, P, LANES], BF16, name="w2_bf", align_bytes=64)
-        for side, engine_copy in enumerate((nc.vector.tensor_copy, nc.scalar.copy)):
+        for side, engine_copy in enumerate((nc.scalar.copy, nc.vector.tensor_copy)):
             engine_copy(w2_bf[:, :, side * P // 2 : (side + 1) * P // 2, :].rearrange("p t m j -> p m t j"), dealt(w2_raw[side]))
-        y_rest = keep.tile([P, 3 * S], F32, name="y_rest", tag="w2_raw1")
-        y.extend([product(w1_ops[t], y_rest[:, (t - 1) * S : t * S]) for t in range(1, LANES)])
+        y_all = keep.tile([P, LANES * S], F32, name="y_all", tag="w2_raw0")
+        y = [product(w1_ops[t], y_all[:, t * S : (t + 1) * S], pieces=2 if t == 0 else 1) for t in range(LANES)]
+        centre = keep.tile([P, LANES, V], F32, name="centre", tag="w2_raw1")
+        nc.vector.tensor_copy(centre[:, 0, :], y[0].indirect(cen_list[:]))
         w2_ops = quantise(w2_bf, "w2")
-        centre = keep.tile([P, LANES, V], F32, name="centre", tag="w2_raw0")
-        for t in range(LANES):
-            nc.vector.tensor_copy(centre[:, t, :], y[t][:].indirect(cen_list[:]))
+        for t in range(1, LANES):
+            nc.vector.tensor_copy(centre[:, t, :], y[t].indirect(cen_list[:]))
         e = [product(w2_ops[t], keep.tile([P, S], F32, name=f"e{t}")) for t in range(LANES)]
 
         edge_bf = [keep.tile([P, 2, V, 2], BF16, name=f"edge_bf{d}") for d in range(3)]

@@ -24,8 +24,9 @@ S_HALF = S // 2
 V_HALF = V // 2
 LOW, HIGH = slice(0, 2), slice(2, 4)
 SCALAR_PLACES = 80
-PRODUCT_BANKS = 5
-OUT_BANKS = 3
+EDGE_TILES = 4
+PRODUCT_BANKS = 4
+OUT_BANKS = 4
 
 
 def tile_picked_edgecv_relu_e_kernel(tc, xT, w1, w2, w3_words, w3_scales, offs, cen, pos1, pos2, pos3, out):
@@ -87,11 +88,6 @@ def tile_picked_edgecv_relu_e_kernel(tc, xT, w1, w2, w3_words, w3_scales, offs, 
         def dealt(raw):
             return raw[:].rearrange("p j (m t) -> p m t j", t=LANES)
 
-        def deal(engine_copy, raw, lanes, tag):
-            w_bf = keep.tile([P, lanes.stop - lanes.start, P, LANES], BF16, name=tag, tag=tag, align_bytes=64)
-            engine_copy(w_bf[:].rearrange("p t m j -> p m t j"), dealt(raw)[:, :, lanes, :])
-            return w_bf
-
         def quantise(w_bf, name):
             count = w_bf.shape[1]
             codes = keep.tile([P, count * P], U32, name=f"{name}_codes", align_bytes=64)
@@ -136,34 +132,29 @@ def tile_picked_edgecv_relu_e_kernel(tc, xT, w1, w2, w3_words, w3_scales, offs, 
         larger = keep.tile([P, 2, V, 2], BF16, name="larger")
         for u in range(2):
             for d in range(3):
-                edge = keep.tile([P, 2, V], F32, name=f"edge{u}{d}", tag=f"edge{(3 * u + d) % 4}")
+                edge = keep.tile([P, 2, V], F32, name=f"edge{u}{d}", tag=f"edge{(3 * u + d) % EDGE_TILES}")
                 pieces = 2 if (u, d) == (1, 2) else 1
                 width = V // pieces
                 for h in range(pieces):
                     cols = slice(h * width, (h + 1) * width)
                     entries = pos_lists[d][:, h * width // GROUP : (h + 1) * width // GROUP]
-                    for i in range(2):
-                        nc.vector.tensor_tensor(edge[:, i, cols], e[2 * u + i][:].indirect(entries), centre[:, 2 * u + i, cols], ALU.add)
-                    nc.scalar.activation(edge_bf[d][:, u, cols, :], edge[:, :, cols].rearrange("p t v -> p v t"), ACT.Relu)
+                    for s in range(2):
+                        nc.vector.tensor_tensor(edge[:, s, cols], e[2 * u + s][:].indirect(entries), centre[:, 2 * u + s, cols], ALU.add)
+                    nc.scalar.activation(edge_bf[d][:, u, cols, :], edge[:, :, cols].rearrange("p s v -> p v s"), ACT.Relu)
 
         out_rows = out.rearrange("(a p) v -> p a v", p=P)
-
-        def flat(tile, h):
-            return tile[:, h * V_HALF : (h + 1) * V_HALF, :].rearrange("p v t -> p (v t)")
-
-        z_all = keep.tile([P, V, LANES], BF16, name="z_all", align_bytes=64)
-        for h in range(2):
-            cols = slice(h * V_HALF, (h + 1) * V_HALF)
+        halves = [slice(h * V_HALF, (h + 1) * V_HALF) for h in range(2)]
+        z_bf = keep.tile([P, V, LANES], BF16, name="z_bf", align_bytes=64)
+        for cols in halves:
             nc.vector.tensor_tensor(larger[:, :, cols, :], edge_bf[0][:, :, cols, :], edge_bf[1][:, :, cols, :], ALU.max)
-        for h in range(2):
-            cols = slice(h * V_HALF, (h + 1) * V_HALF)
-            woven = [tile[:, :, cols, :].rearrange("p u v t -> p v u t") for tile in (larger, edge_bf[2])]
-            nc.vector.tensor_tensor(z_all[:, cols, :].rearrange("p v (u t) -> p v u t", u=2), woven[0], woven[1], ALU.max)
+        for cols in halves:
+            woven = [tile[:, :, cols, :].rearrange("p u v s -> p v u s") for tile in (larger, edge_bf[2])]
+            nc.vector.tensor_tensor(z_bf[:, cols, :].rearrange("p v (u s) -> p v u s", u=2), woven[0], woven[1], ALU.max)
 
         def quantise_z(h):
             codes = keep.tile([P, V_HALF], U32, name=f"z_codes{h}", align_bytes=64)
             scale = keep.tile([P, V_HALF], U8, name=f"z_scale{h}", align_bytes=64)
-            nc.vector.quantize_mx(out=codes[:].bitcast(FP8X4), scales=scale[:], in_=flat(z_all, h))
+            nc.vector.quantize_mx(out=codes[:].bitcast(FP8X4), scales=scale[:], in_=z_bf[:, halves[h], :].rearrange("p v t -> p (v t)"))
             return codes, scale
 
         def project(dst, a, z_op):
@@ -177,18 +168,11 @@ def tile_picked_edgecv_relu_e_kernel(tc, xT, w1, w2, w3_words, w3_scales, offs, 
                 stop=True,
             )
 
-        z_op = quantise_z(0)
-        out_bank = out_psum.tile([P, 2, V_HALF], F32, name="out_bank")
-        for a in range(2):
-            project(out_bank[:, a, :], a, z_op)
-        staged = keep.tile([P, 2, V_HALF], F32, name="staged_first")
-        nc.scalar.copy(staged[:], out_bank[:])
-        nc.sync.dma_start(out_rows[:, :, 0:V_HALF], staged[:])
-
-        z_op = quantise_z(1)
-        for a, (engine_copy, queue) in enumerate(((nc.vector.tensor_copy, nc.sync), (nc.scalar.copy, nc.scalar))):
-            out_bank = out_psum.tile([P, 2, V_HALF], F32, name="out_bank")
-            project(out_bank[:, 0, :], a, z_op)
-            staged = keep.tile([P, V_HALF], F32, name=f"staged_second{a}")
-            engine_copy(staged[:], out_bank[:, 0, :])
-            queue.dma_start(out_rows[:, a, V_HALF:V], staged[:])
+        for h, cols in enumerate(halves):
+            z_op = quantise_z(h)
+            for a, (engine_copy, queue) in enumerate(((nc.vector.tensor_copy, nc.sync), (nc.scalar.copy, nc.scalar))):
+                out_bank = out_psum.tile([P, V_HALF], F32, name="out_bank")
+                project(out_bank[:], a, z_op)
+                staged = keep.tile([P, V_HALF], F32, name=f"staged{h}{a}")
+                engine_copy(staged[:], out_bank[:])
+                queue.dma_start(out_rows[:, a, cols], staged[:])

@@ -23,7 +23,7 @@ QUADRANT = 32
 S_HALF = S // 2
 V_HALF = V // 2
 LOW, HIGH = slice(0, 2), slice(2, 4)
-SCALAR_PLACES = 80
+SCALAR_PLACES = 44
 EDGE_TILES = 4
 PRODUCT_BANKS = 4
 OUT_BANKS = 4
@@ -67,7 +67,6 @@ def tile_picked_edgecv_relu_e_kernel(tc, xT, w1, w2, w3_words, w3_scales, offs, 
 
         x_bf = [keep.tile([P, S_HALF, LANES], BF16, name=f"x_bf{h}", align_bytes=64) for h in range(2)]
         picked_low = keep.tile([P, 2, S], F32, name="picked_low")
-        picked_high = [keep.tile([P, 2, S_HALF], F32, name=f"picked_high{h}") for h in range(2)]
         for j in range(2):
             nc.vector.tensor_copy(picked_low[:, j, :], x_lane[j][:].indirect(offs_list[:]))
         for h in range(2):
@@ -76,9 +75,7 @@ def tile_picked_edgecv_relu_e_kernel(tc, xT, w1, w2, w3_words, w3_scales, offs, 
         for j in range(2):
             for h in range(2):
                 entries = offs_list[:, h * half_columns : (h + 1) * half_columns]
-                nc.vector.tensor_copy(picked_high[h][:, j, :], x_lane[2 + j][:].indirect(entries))
-        nc.scalar.copy(x_bf[0][:, :, HIGH], picked_high[0][:].rearrange("p j s -> p s j"))
-        nc.vector.tensor_copy(x_bf[1][:, :, HIGH], picked_high[1][:].rearrange("p j s -> p s j"))
+                nc.vector.tensor_copy(x_bf[h][:, :, 2 + j], x_lane[2 + j][:].indirect(entries))
         x_codes = keep.tile([P, S], U32, name="x_codes", align_bytes=64)
         x_scale = keep.tile([P, S], U8, name="x_scale", align_bytes=64)
         for h in range(2):

@@ -83,7 +83,7 @@ def tile_picked_edgecv_relu_e_kernel(tc, xT, w1, w2, w3_words, w3_scales, offs, 
             nc.vector.quantize_mx(out=x_codes[:, cols].bitcast(FP8X4), scales=x_scale[:, cols], in_=x_bf[h][:].rearrange("p s j -> p (s j)"))
 
         def dealt(raw):
-            return raw[:].rearrange("p j (m t) -> p m t j", t=LANES)
+            return raw[:].rearrange("p j (m t) -> p m j t", t=LANES)
 
         def quantise(w_bf, name):
             count = w_bf.shape[1]
@@ -111,11 +111,11 @@ def tile_picked_edgecv_relu_e_kernel(tc, xT, w1, w2, w3_words, w3_scales, offs, 
 
         w1_bf = keep.tile([P, LANES, P, LANES], BF16, name="w1_bf", align_bytes=64)
         for places, engine_copy in ((slice(0, SCALAR_PLACES), nc.scalar.copy), (slice(SCALAR_PLACES, P), nc.vector.tensor_copy)):
-            engine_copy(w1_bf[:, :, places, :].rearrange("p t m j -> p m t j"), dealt(w1_raw)[:, places])
+            engine_copy(w1_bf[:, :, places, :].rearrange("p t m j -> p m j t"), dealt(w1_raw)[:, places])
         w1_ops = quantise(w1_bf[:, LOW], "w1_low") + quantise(w1_bf[:, HIGH], "w1_high")
         w2_bf = keep.tile([P, LANES, P, LANES], BF16, name="w2_bf", align_bytes=64)
         for side, engine_copy in enumerate((nc.scalar.copy, nc.vector.tensor_copy)):
-            engine_copy(w2_bf[:, :, side * P // 2 : (side + 1) * P // 2, :].rearrange("p t m j -> p m t j"), dealt(w2_raw[side]))
+            engine_copy(w2_bf[:, :, side * P // 2 : (side + 1) * P // 2, :].rearrange("p t m j -> p m j t"), dealt(w2_raw[side]))
         y_all = keep.tile([P, LANES * S], F32, name="y_all", tag="w2_raw0")
         y = [product(w1_ops[t], y_all[:, t * S : (t + 1) * S], pieces=2 if t == 0 else 1) for t in range(LANES)]
         centre = keep.tile([P, LANES, V], F32, name="centre", tag="w2_raw1")

@@ -24,6 +24,8 @@ S_HALF = S // 2
 V_HALF = V // 2
 LOW, HIGH = slice(0, 2), slice(2, 4)
 SCALAR_PLACES = 44
+W2_FIRST_PLACES = 96
+W2_SCALAR_PLACES = 44
 EDGE_TILES = 4
 PRODUCT_BANKS = 4
 OUT_BANKS = 4
@@ -52,9 +54,13 @@ def tile_picked_edgecv_relu_e_kernel(tc, xT, w1, w2, w3_words, w3_scales, offs, 
         w1_raw = keep.tile([P, LANES, H], F32, name="w1_raw")
         for pair in (LOW, HIGH):
             nc.sync.dma_start(w1_raw[:, pair, :], w1.rearrange("(p j) c -> p j c", j=LANES)[:, pair, :])
-        w2_raw = [keep.tile([P, LANES, H // 2], F32, name=f"w2_raw{side}", tag=f"w2_raw{side}") for side in range(2)]
-        for side in range(2):
-            nc.sync.dma_start(w2_raw[side][:], w2.rearrange("(p j) (s c) -> p s j c", j=LANES, s=2)[:, side])
+        w2_rows = w2.rearrange("(p j) c -> p j c", j=LANES)
+        w2_cut = LANES * W2_FIRST_PLACES
+        w2_raw = []
+        for side, cols in enumerate((slice(0, w2_cut), slice(w2_cut, H))):
+            raw = keep.tile([P, LANES, cols.stop - cols.start], F32, name=f"w2_raw{side}", tag=f"w2_raw{side}")
+            nc.sync.dma_start(raw[:], w2_rows[:, :, cols])
+            w2_raw.append(raw)
         cen_list = load_list(cen, V, "cen_list")
         pos_lists = [load_list(src, V, f"pos_list{d}") for d, src in enumerate((pos1, pos2, pos3))]
 
@@ -114,14 +120,15 @@ def tile_picked_edgecv_relu_e_kernel(tc, xT, w1, w2, w3_words, w3_scales, offs, 
             engine_copy(w1_bf[:, :, places, :].rearrange("p t m j -> p m j t"), dealt(w1_raw)[:, places])
         w1_ops = quantise(w1_bf[:, LOW], "w1_low") + quantise(w1_bf[:, HIGH], "w1_high")
         w2_bf = keep.tile([P, LANES, P, LANES], BF16, name="w2_bf", align_bytes=64)
-        for side, engine_copy in enumerate((nc.scalar.copy, nc.vector.tensor_copy)):
-            engine_copy(w2_bf[:, :, side * P // 2 : (side + 1) * P // 2, :].rearrange("p t m j -> p m j t"), dealt(w2_raw[side]))
+        w2_dst = w2_bf[:].rearrange("p t m j -> p m j t")
+        nc.scalar.copy(w2_dst[:, 0:W2_SCALAR_PLACES], dealt(w2_raw[0])[:, 0:W2_SCALAR_PLACES])
+        nc.vector.tensor_copy(w2_dst[:, W2_SCALAR_PLACES:W2_FIRST_PLACES], dealt(w2_raw[0])[:, W2_SCALAR_PLACES:W2_FIRST_PLACES])
+        nc.vector.tensor_copy(w2_dst[:, W2_FIRST_PLACES:P], dealt(w2_raw[1]))
         y_all = keep.tile([P, LANES * S], F32, name="y_all", tag="w2_raw0")
         y = [product(w1_ops[t], y_all[:, t * S : (t + 1) * S], pieces=2 if t == 0 else 1) for t in range(LANES)]
         centre = keep.tile([P, LANES, V], F32, name="centre", tag="w2_raw1")
-        nc.vector.tensor_copy(centre[:, 0, :], y[0].indirect(cen_list[:]))
         w2_ops = quantise(w2_bf, "w2")
-        for t in range(1, LANES):
+        for t in range(LANES):
             nc.vector.tensor_copy(centre[:, t, :], y[t].indirect(cen_list[:]))
         e = [product(w2_ops[t], keep.tile([P, S], F32, name=f"e{t}")) for t in range(LANES)]
 

@@ -23,9 +23,15 @@ QUADRANT = 32
 S_HALF = S // 2
 V_HALF = V // 2
 LOW, HIGH = slice(0, 2), slice(2, 4)
-SCALAR_PLACES = 44
+W1_SCALAR_PLACES = 56
 W2_FIRST_PLACES = 96
-W2_SCALAR_PLACES = 44
+W2_SCALAR_PLACES = 32
+Y_BYTES = 4 * LANES * S
+Y_AT = 0
+W2_FIRST_AT = Y_BYTES // 2
+W1_HIGH_CODES_AT = Y_BYTES
+W1_LOW_CODES_AT = W2_FIRST_AT + Y_BYTES
+W2_CODES_AT = W1_LOW_CODES_AT + Y_BYTES // 4
 EDGE_TILES = 4
 PRODUCT_BANKS = 4
 OUT_BANKS = 4
@@ -36,6 +42,7 @@ def tile_picked_edgecv_relu_e_kernel(tc, xT, w1, w2, w3_words, w3_scales, offs, 
     with ExitStack() as ctx:
         lists = ctx.enter_context(tc.tile_pool(name="lists", bufs=1))
         keep = ctx.enter_context(tc.tile_pool(name="keep", bufs=1))
+        placed = ctx.enter_context(tc.tile_pool(name="placed", bufs=1))
         product_psum = ctx.enter_context(tc.psum_pool(name="product_psum", bufs=PRODUCT_BANKS))
         out_psum = ctx.enter_context(tc.psum_pool(name="out_psum", bufs=OUT_BANKS))
 
@@ -52,15 +59,15 @@ def tile_picked_edgecv_relu_e_kernel(tc, xT, w1, w2, w3_words, w3_scales, offs, 
             nc.sync.dma_start(x_lane[j][:], x_rows[:, j, :])
 
         w1_raw = keep.tile([P, LANES, H], F32, name="w1_raw")
-        for pair in (LOW, HIGH):
-            nc.sync.dma_start(w1_raw[:, pair, :], w1.rearrange("(p j) c -> p j c", j=LANES)[:, pair, :])
+        w1_cut = LANES * H - H // 2
+        for run in (slice(0, w1_cut), slice(w1_cut, LANES * H)):
+            nc.sync.dma_start(w1_raw[:].rearrange("p j c -> p (j c)")[:, run], w1.rearrange("(p j) c -> p (j c)", j=LANES)[:, run])
         w2_rows = w2.rearrange("(p j) c -> p j c", j=LANES)
         w2_cut = LANES * W2_FIRST_PLACES
-        w2_raw = []
-        for side, cols in enumerate((slice(0, w2_cut), slice(w2_cut, H))):
-            raw = keep.tile([P, LANES, cols.stop - cols.start], F32, name=f"w2_raw{side}", tag=f"w2_raw{side}")
-            nc.sync.dma_start(raw[:], w2_rows[:, :, cols])
-            w2_raw.append(raw)
+        w2_first = placed.tile([P, LANES, w2_cut], F32, name="w2_raw0", offset=W2_FIRST_AT, align_bytes=64)
+        nc.sync.dma_start(w2_first[:], w2_rows[:, :, 0:w2_cut])
+        w2_last = keep.tile([P, LANES, H - w2_cut], F32, name="w2_raw1", tag="w2_last")
+        nc.sync.dma_start(w2_last[:], w2_rows[:, :, w2_cut:H])
         cen_list = load_list(cen, V, "cen_list")
         pos_lists = [load_list(src, V, f"pos_list{d}") for d, src in enumerate((pos1, pos2, pos3))]
 
@@ -91,43 +98,41 @@ def tile_picked_edgecv_relu_e_kernel(tc, xT, w1, w2, w3_words, w3_scales, offs, 
         def dealt(raw):
             return raw[:].rearrange("p j (m t) -> p m j t", t=LANES)
 
-        def quantise(w_bf, name):
+        def quantise(w_bf, name, offset):
             count = w_bf.shape[1]
-            codes = keep.tile([P, count * P], U32, name=f"{name}_codes", align_bytes=64)
+            codes = placed.tile([P, count * P], U32, name=f"{name}_codes", offset=offset, align_bytes=64)
             scale = keep.tile([P, count * P], U8, name=f"{name}_scale", align_bytes=64)
             nc.vector.quantize_mx(out=codes[:].bitcast(FP8X4), scales=scale[:], in_=w_bf[:].rearrange("p t m j -> p (t m j)"))
             return [(codes[:, i * P : (i + 1) * P], scale[:, i * P : (i + 1) * P]) for i in range(count)]
 
-        def product(weights, rows, pieces=1):
-            width = S // pieces
-            for i in range(pieces):
-                cols = slice(i * width, (i + 1) * width)
-                bank = product_psum.tile([P, S], F32, name="bank")
-                nc.tensor.matmul_mx(
-                    out=bank[:, 0:width],
-                    lhsT=weights[0].bitcast(FP8X4),
-                    lhsT_scale=weights[1],
-                    rhs=x_codes[:, cols].bitcast(FP8X4),
-                    rhs_scale=x_scale[:, cols],
-                    start=True,
-                    stop=True,
-                )
-                nc.scalar.copy(rows[:, cols], bank[:, 0:width])
+        def product(weights, rows):
+            bank = product_psum.tile([P, S], F32, name="bank")
+            nc.tensor.matmul_mx(
+                out=bank[:],
+                lhsT=weights[0].bitcast(FP8X4),
+                lhsT_scale=weights[1],
+                rhs=x_codes[:].bitcast(FP8X4),
+                rhs_scale=x_scale[:],
+                start=True,
+                stop=True,
+            )
+            nc.scalar.copy(rows[:], bank[:])
             return rows
 
         w1_bf = keep.tile([P, LANES, P, LANES], BF16, name="w1_bf", align_bytes=64)
-        for places, engine_copy in ((slice(0, SCALAR_PLACES), nc.scalar.copy), (slice(SCALAR_PLACES, P), nc.vector.tensor_copy)):
+        for places, engine_copy in ((slice(0, W1_SCALAR_PLACES), nc.scalar.copy), (slice(W1_SCALAR_PLACES, P), nc.vector.tensor_copy)):
             engine_copy(w1_bf[:, :, places, :].rearrange("p t m j -> p m j t"), dealt(w1_raw)[:, places])
-        w1_ops = quantise(w1_bf[:, LOW], "w1_low") + quantise(w1_bf[:, HIGH], "w1_high")
+        w1_ops = quantise(w1_bf[:, LOW], "w1_low", W1_LOW_CODES_AT)
         w2_bf = keep.tile([P, LANES, P, LANES], BF16, name="w2_bf", align_bytes=64)
         w2_dst = w2_bf[:].rearrange("p t m j -> p m j t")
-        nc.scalar.copy(w2_dst[:, 0:W2_SCALAR_PLACES], dealt(w2_raw[0])[:, 0:W2_SCALAR_PLACES])
-        nc.vector.tensor_copy(w2_dst[:, W2_SCALAR_PLACES:W2_FIRST_PLACES], dealt(w2_raw[0])[:, W2_SCALAR_PLACES:W2_FIRST_PLACES])
-        nc.vector.tensor_copy(w2_dst[:, W2_FIRST_PLACES:P], dealt(w2_raw[1]))
-        y_all = keep.tile([P, LANES * S], F32, name="y_all", tag="w2_raw0")
-        y = [product(w1_ops[t], y_all[:, t * S : (t + 1) * S], pieces=2 if t == 0 else 1) for t in range(LANES)]
-        centre = keep.tile([P, LANES, V], F32, name="centre", tag="w2_raw1")
-        w2_ops = quantise(w2_bf, "w2")
+        nc.scalar.copy(w2_dst[:, 0:W2_SCALAR_PLACES], dealt(w2_first)[:, 0:W2_SCALAR_PLACES])
+        nc.vector.tensor_copy(w2_dst[:, W2_SCALAR_PLACES:W2_FIRST_PLACES], dealt(w2_first)[:, W2_SCALAR_PLACES:W2_FIRST_PLACES])
+        nc.vector.tensor_copy(w2_dst[:, W2_FIRST_PLACES:P], dealt(w2_last))
+        w1_ops = w1_ops + quantise(w1_bf[:, HIGH], "w1_high", W1_HIGH_CODES_AT)
+        y_all = placed.tile([P, LANES * S], F32, name="y_all", offset=Y_AT, align_bytes=64)
+        y = [product(w1_ops[t], y_all[:, t * S : (t + 1) * S]) for t in range(LANES)]
+        centre = keep.tile([P, LANES, V], F32, name="centre", tag="w2_last")
+        w2_ops = quantise(w2_bf, "w2", W2_CODES_AT)
         for t in range(LANES):
             nc.vector.tensor_copy(centre[:, t, :], y[t].indirect(cen_list[:]))
         e = [product(w2_ops[t], keep.tile([P, S], F32, name=f"e{t}")) for t in range(LANES)]

@@ -18,23 +18,27 @@ ACT = mybir.ActivationFunctionType
 
 P = 128
 LANES = 4
+LAST = LANES - 1
 GROUP = 16
 QUADRANT = 32
 S_HALF = S // 2
 V_HALF = V // 2
+ALL_POINTS = slice(0, S)
+POINT_HALVES = (slice(0, S_HALF), slice(S_HALF, S))
+CENTRE_HALVES = (slice(0, V_HALF), slice(V_HALF, V))
 LOW, HIGH = slice(0, 2), slice(2, 4)
-W1_SCALAR_PLACES = 56
-W2_FIRST_PLACES = 96
-W2_SCALAR_PLACES = 32
-Y_BYTES = 4 * LANES * S
-Y_AT = 0
-W2_FIRST_AT = Y_BYTES // 2
-W1_HIGH_CODES_AT = Y_BYTES
-W1_LOW_CODES_AT = W2_FIRST_AT + Y_BYTES
-W2_CODES_AT = W1_LOW_CODES_AT + Y_BYTES // 4
-EDGE_TILES = 4
-PRODUCT_BANKS = 4
-OUT_BANKS = 4
+X_FEW = 64
+W2_LEFT_SCALAR_PLACES = 24
+W2_RIGHT_SCALAR_PLACES = 20
+W1_FIRST_PLACES = 96
+ROW_BYTES = 4 * S
+CENTRE_BYTES = 4 * V
+W1_FIRST_AT = 0
+W1_LAST_AT = W1_FIRST_AT + 4 * LANES * LANES * W1_FIRST_PLACES
+W1_BF_AT = W1_FIRST_AT + 4 * LANES * H
+LARGEST_AT = W1_BF_AT + 2 * LANES * H
+PICKED_AT = LARGEST_AT + LANES * CENTRE_BYTES
+Y_BANK = LANES
 
 
 def tile_picked_edgecv_relu_e_kernel(tc, xT, w1, w2, w3_words, w3_scales, offs, cen, pos1, pos2, pos3, out):
@@ -43,13 +47,21 @@ def tile_picked_edgecv_relu_e_kernel(tc, xT, w1, w2, w3_words, w3_scales, offs, 
         lists = ctx.enter_context(tc.tile_pool(name="lists", bufs=1))
         keep = ctx.enter_context(tc.tile_pool(name="keep", bufs=1))
         placed = ctx.enter_context(tc.tile_pool(name="placed", bufs=1))
-        product_psum = ctx.enter_context(tc.psum_pool(name="product_psum", bufs=PRODUCT_BANKS))
-        out_psum = ctx.enter_context(tc.psum_pool(name="out_psum", bufs=OUT_BANKS))
+        psum = ctx.enter_context(tc.psum_pool(name="psum", bufs=1))
 
         def load_list(src, entries, name):
             tile = lists.tile([P, entries // GROUP], U16, name=name)
             nc.sync.dma_start(tile[:], src)
             return tile
+
+        def entries_of(list_tile, start, stop):
+            return list_tile[:, start // GROUP : stop // GROUP]
+
+        def place(shape, dtype, name, offset):
+            return placed.tile(shape, dtype, name=name, offset=offset, align_bytes=64)
+
+        def scalar_gather(dst, window):
+            nc.scalar.activation(dst, window, ACT.Copy)
 
         x_rows = xT.rearrange("(p j) c -> p j c", j=LANES)
         x_lane = [keep.tile([P, T], F32, name=f"x_lane{j}") for j in range(LANES)]
@@ -58,18 +70,18 @@ def tile_picked_edgecv_relu_e_kernel(tc, xT, w1, w2, w3_words, w3_scales, offs, 
         for j in range(1, LANES):
             nc.sync.dma_start(x_lane[j][:], x_rows[:, j, :])
 
-        w1_raw = keep.tile([P, LANES, H], F32, name="w1_raw")
-        w1_cut = LANES * H - H // 2
-        for run in (slice(0, w1_cut), slice(w1_cut, LANES * H)):
-            nc.sync.dma_start(w1_raw[:].rearrange("p j c -> p (j c)")[:, run], w1.rearrange("(p j) c -> p (j c)", j=LANES)[:, run])
-        w2_rows = w2.rearrange("(p j) c -> p j c", j=LANES)
-        w2_cut = LANES * W2_FIRST_PLACES
-        w2_first = placed.tile([P, LANES, w2_cut], F32, name="w2_raw0", offset=W2_FIRST_AT, align_bytes=64)
-        nc.sync.dma_start(w2_first[:], w2_rows[:, :, 0:w2_cut])
-        w2_last = keep.tile([P, LANES, H - w2_cut], F32, name="w2_raw1", tag="w2_last")
-        nc.sync.dma_start(w2_last[:], w2_rows[:, :, w2_cut:H])
-        cen_list = load_list(cen, V, "cen_list")
+        w2_raw = keep.tile([P, LANES, H], F32, name="w2_raw")
+        w2_cut = LANES * H - H // 2
+        for run in (slice(0, w2_cut), slice(w2_cut, LANES * H)):
+            nc.sync.dma_start(w2_raw[:].rearrange("p j c -> p (j c)")[:, run], w2.rearrange("(p j) c -> p (j c)", j=LANES)[:, run])
         pos_lists = [load_list(src, V, f"pos_list{d}") for d, src in enumerate((pos1, pos2, pos3))]
+        w1_rows = w1.rearrange("(p j) c -> p j c", j=LANES)
+        w1_cut = LANES * W1_FIRST_PLACES
+        w1_first = place([P, LANES, w1_cut], F32, "w1_first", W1_FIRST_AT)
+        nc.sync.dma_start(w1_first[:], w1_rows[:, :, 0:w1_cut])
+        w1_last = place([P, LANES, H - w1_cut], F32, "w1_last", W1_LAST_AT)
+        nc.sync.dma_start(w1_last[:], w1_rows[:, :, w1_cut:H])
+        cen_list = load_list(cen, V, "cen_list")
 
         w3_codes = keep.tile([P, 2 * N], U8, name="w3_codes", align_bytes=64)
         nc.sync.dma_start(w3_codes[:].bitcast(I32), w3_words[0].bitcast(I32))
@@ -79,109 +91,149 @@ def tile_picked_edgecv_relu_e_kernel(tc, xT, w1, w2, w3_words, w3_scales, offs, 
             nc.sync.dma_start(w3_scale[QUADRANT * q : QUADRANT * q + 4, :].bitcast(I32), w3_scales[0, 4 * q : 4 * q + 4, :].bitcast(I32))
 
         x_bf = [keep.tile([P, S_HALF, LANES], BF16, name=f"x_bf{h}", align_bytes=64) for h in range(2)]
-        picked_low = keep.tile([P, 2, S], F32, name="picked_low")
-        for j in range(2):
-            nc.vector.tensor_copy(picked_low[:, j, :], x_lane[j][:].indirect(offs_list[:]))
-        for h in range(2):
-            nc.scalar.copy(x_bf[h][:, :, LOW], picked_low[:, :, h * S_HALF : (h + 1) * S_HALF].rearrange("p j s -> p s j"))
-        half_columns = S_HALF // GROUP
-        for j in range(2):
-            for h in range(2):
-                entries = offs_list[:, h * half_columns : (h + 1) * half_columns]
-                nc.vector.tensor_copy(x_bf[h][:, :, 2 + j], x_lane[2 + j][:].indirect(entries))
+        few, rest = slice(0, X_FEW), slice(X_FEW, S_HALF)
+        picked = place([P, LANES, S_HALF], F32, "picked", PICKED_AT)
+        first_few = place([P, X_FEW], F32, "first_few", PICKED_AT + 4 * X_FEW)
+        nc.vector.tensor_copy(first_few[:], x_lane[0][:].indirect(entries_of(offs_list, S_HALF, S_HALF + X_FEW)))
+        nc.scalar.copy(x_bf[1][:, few, 0], first_few[:])
+        scalar_gather(picked[:, 0, rest], x_lane[0][:].indirect(entries_of(offs_list, S_HALF + X_FEW, S)))
+        for j in range(LANES):
+            nc.vector.tensor_copy(x_bf[0][:, :, j], x_lane[j][:].indirect(entries_of(offs_list, 0, S_HALF)))
+        for j in (1, 2):
+            scalar_gather(picked[:, j, :], x_lane[j][:].indirect(entries_of(offs_list, S_HALF, S)))
+        nc.scalar.copy(x_bf[1][:, rest, LOW], picked[:, LOW, rest].rearrange("p j s -> p s j"))
+        scalar_gather(picked[:, LAST, :], x_lane[LAST][:].indirect(entries_of(offs_list, S_HALF, S)))
+        nc.vector.tensor_copy(x_bf[1][:, rest, HIGH], picked[:, HIGH, rest].rearrange("p j s -> p s j"))
+        nc.vector.tensor_copy(x_bf[1][:, few, 1:LANES], picked[:, 1:LANES, few].rearrange("p j s -> p s j"))
         x_codes = keep.tile([P, S], U32, name="x_codes", align_bytes=64)
         x_scale = keep.tile([P, S], U8, name="x_scale", align_bytes=64)
-        for h in range(2):
-            cols = slice(h * S_HALF, (h + 1) * S_HALF)
+        for h, cols in enumerate(POINT_HALVES):
             nc.vector.quantize_mx(out=x_codes[:, cols].bitcast(FP8X4), scales=x_scale[:, cols], in_=x_bf[h][:].rearrange("p s j -> p (s j)"))
 
         def dealt(raw):
             return raw[:].rearrange("p j (m t) -> p m j t", t=LANES)
 
-        def quantise(w_bf, name, offset):
+        def quantise(w_bf, name):
             count = w_bf.shape[1]
-            codes = placed.tile([P, count * P], U32, name=f"{name}_codes", offset=offset, align_bytes=64)
+            codes = keep.tile([P, count * P], U32, name=f"{name}_codes", align_bytes=64)
             scale = keep.tile([P, count * P], U8, name=f"{name}_scale", align_bytes=64)
             nc.vector.quantize_mx(out=codes[:].bitcast(FP8X4), scales=scale[:], in_=w_bf[:].rearrange("p t m j -> p (t m j)"))
             return [(codes[:, i * P : (i + 1) * P], scale[:, i * P : (i + 1) * P]) for i in range(count)]
 
-        def product(weights, rows):
-            bank = product_psum.tile([P, S], F32, name="bank")
+        def product(weights, bank_no, cols):
+            bank = psum.tile([P, cols.stop - cols.start], F32, name=f"bank{bank_no}", tag=f"bank{bank_no}")
             nc.tensor.matmul_mx(
                 out=bank[:],
                 lhsT=weights[0].bitcast(FP8X4),
                 lhsT_scale=weights[1],
-                rhs=x_codes[:].bitcast(FP8X4),
-                rhs_scale=x_scale[:],
+                rhs=x_codes[:, cols].bitcast(FP8X4),
+                rhs_scale=x_scale[:, cols],
                 start=True,
                 stop=True,
             )
-            nc.scalar.copy(rows[:], bank[:])
-            return rows
+            return bank
 
-        w1_bf = keep.tile([P, LANES, P, LANES], BF16, name="w1_bf", align_bytes=64)
-        for places, engine_copy in ((slice(0, W1_SCALAR_PLACES), nc.scalar.copy), (slice(W1_SCALAR_PLACES, P), nc.vector.tensor_copy)):
-            engine_copy(w1_bf[:, :, places, :].rearrange("p t m j -> p m j t"), dealt(w1_raw)[:, places])
-        w1_ops = quantise(w1_bf[:, LOW], "w1_low", W1_LOW_CODES_AT)
         w2_bf = keep.tile([P, LANES, P, LANES], BF16, name="w2_bf", align_bytes=64)
         w2_dst = w2_bf[:].rearrange("p t m j -> p m j t")
-        nc.scalar.copy(w2_dst[:, 0:W2_SCALAR_PLACES], dealt(w2_first)[:, 0:W2_SCALAR_PLACES])
-        nc.vector.tensor_copy(w2_dst[:, W2_SCALAR_PLACES:W2_FIRST_PLACES], dealt(w2_first)[:, W2_SCALAR_PLACES:W2_FIRST_PLACES])
-        nc.vector.tensor_copy(w2_dst[:, W2_FIRST_PLACES:P], dealt(w2_last))
-        w1_ops = w1_ops + quantise(w1_bf[:, HIGH], "w1_high", W1_HIGH_CODES_AT)
-        y_all = placed.tile([P, LANES * S], F32, name="y_all", offset=Y_AT, align_bytes=64)
-        y = [product(w1_ops[t], y_all[:, t * S : (t + 1) * S]) for t in range(LANES)]
-        centre = keep.tile([P, LANES, V], F32, name="centre", tag="w2_last")
-        w2_ops = quantise(w2_bf, "w2", W2_CODES_AT)
-        for t in range(LANES):
-            nc.vector.tensor_copy(centre[:, t, :], y[t].indirect(cen_list[:]))
-        e = [product(w2_ops[t], keep.tile([P, S], F32, name=f"e{t}")) for t in range(LANES)]
+        for start, scalar_places in ((0, W2_LEFT_SCALAR_PLACES), (P // 2, W2_RIGHT_SCALAR_PLACES)):
+            cut, stop = start + scalar_places, start + P // 2
+            nc.scalar.copy(w2_dst[:, start:cut], dealt(w2_raw)[:, start:cut])
+            nc.vector.tensor_copy(w2_dst[:, cut:stop], dealt(w2_raw)[:, cut:stop])
+        w2_ops = quantise(w2_bf[:, 0:1], "w2_first") + quantise(w2_bf[:, 1:LANES], "w2_rest")
+        e = [keep.tile([P, S], F32, name=f"e{t}") for t in range(2)]
+        for t in range(2):
+            for cols, bank_no in zip(POINT_HALVES, (t, Y_BANK + LAST - t)):
+                nc.scalar.copy(e[t][:, cols], product(w2_ops[t], bank_no, cols)[:])
+        late_e_banks = [product(w2_ops[t], t, ALL_POINTS) for t in range(2, LANES)]
+        w1_bf = place([P, LANES, P, LANES], BF16, "w1_bf", W1_BF_AT)
+        w1_dst = w1_bf[:].rearrange("p t m j -> p m j t")
+        nc.vector.tensor_copy(w1_dst[:, 0:W1_FIRST_PLACES], dealt(w1_first))
+        nc.vector.tensor_copy(w1_dst[:, W1_FIRST_PLACES:P], dealt(w1_last))
+        w1_ops = quantise(w1_bf, "w1")
+        y_banks = [product(w1_ops[t], Y_BANK + t, ALL_POINTS) for t in range(LAST)]
+        y_last_banks = [product(w1_ops[LAST], bank_no, cols) for cols, bank_no in zip(POINT_HALVES, (0, Y_BANK + LAST))]
 
-        edge_bf = [keep.tile([P, 2, V, 2], BF16, name=f"edge_bf{d}") for d in range(3)]
-        larger = keep.tile([P, 2, V, 2], BF16, name="larger")
-        for u in range(2):
-            for d in range(3):
-                edge = keep.tile([P, 2, V], F32, name=f"edge{u}{d}", tag=f"edge{(3 * u + d) % EDGE_TILES}")
-                pieces = 2 if (u, d) == (1, 2) else 1
-                width = V // pieces
-                for h in range(pieces):
-                    cols = slice(h * width, (h + 1) * width)
-                    entries = pos_lists[d][:, h * width // GROUP : (h + 1) * width // GROUP]
-                    for s in range(2):
-                        nc.vector.tensor_tensor(edge[:, s, cols], e[2 * u + s][:].indirect(entries), centre[:, 2 * u + s, cols], ALU.add)
-                    nc.scalar.activation(edge_bf[d][:, u, cols, :], edge[:, :, cols].rearrange("p s v -> p v s"), ACT.Relu)
+        e = e + [place([P, S], F32, f"e{t}", W1_FIRST_AT + (t - 2) * ROW_BYTES) for t in range(2, LANES)]
+        y = [keep.tile([P, S], F32, name=f"y{t}") for t in range(LANES)]
+        near = [[keep.tile([P, V], F32, name=f"near{t}{d}") for d in range(2)] for t in range(LANES)]
+        for t in range(LANES):
+            name = f"near{t}2"
+            near[t].append(place([P, V], F32, name, W1_LAST_AT + t * CENTRE_BYTES) if t < 2 else keep.tile([P, V], F32, name=name))
+        larger = [place([P, V], F32, f"larger{t}", (W1_BF_AT if t < 2 else LARGEST_AT) + (t % 2) * CENTRE_BYTES) for t in range(LANES)]
+        largest = [place([P, V], F32, f"largest{t}", LARGEST_AT + t * CENTRE_BYTES) for t in range(LANES)]
+        centre = keep.tile([P, V], F32, name="centre")
+        total = keep.tile([P, LANES, V], F32, name="total")
+
+        def fetch(t, d, gather):
+            gather(near[t][d][:], e[t][:].indirect(pos_lists[d][:]))
+
+        def first_max(t):
+            nc.vector.tensor_tensor(larger[t][:], near[t][0][:], near[t][1][:], ALU.max)
+
+        def second_max(t, cols):
+            nc.vector.tensor_tensor(largest[t][:, cols], larger[t][:, cols], near[t][2][:, cols], ALU.max)
+
+        def empty_y(t):
+            nc.vector.tensor_copy(y[t][:], y_banks[t][:])
+
+        def add_centre(t):
+            nc.vector.tensor_tensor(total[:, t, :], y[t][:].indirect(cen_list[:]), largest[t][:], ALU.add)
+
+        for t in range(2):
+            fetch(t, 2, nc.vector.tensor_copy)
+        for t in range(2):
+            for d in range(2):
+                fetch(t, d, scalar_gather)
+            nc.scalar.copy(e[t + 2][:], late_e_banks[t][:])
+        for d in range(3):
+            fetch(2, d, scalar_gather)
+        nc.scalar.copy(y[LAST][:, POINT_HALVES[0]], y_last_banks[0][:])
+        for d in range(3):
+            fetch(LAST, d, scalar_gather)
+        all_centres = slice(0, V)
+        first_max(0)
+        empty_y(0)
+        second_max(0, all_centres)
+        empty_y(1)
+        first_max(1)
+        add_centre(0)
+        second_max(1, all_centres)
+        empty_y(2)
+        nc.vector.tensor_copy(y[LAST][:, POINT_HALVES[1]], y_last_banks[1][:])
+        for cols in CENTRE_HALVES:
+            scalar_gather(centre[:, cols], y[LAST][:].indirect(entries_of(cen_list, cols.start, cols.stop)))
+        first_max(2)
+        add_centre(1)
+        second_max(2, all_centres)
+        first_max(LAST)
+        add_centre(2)
+        for cols in CENTRE_HALVES:
+            second_max(LAST, cols)
+        for cols in CENTRE_HALVES:
+            nc.vector.tensor_tensor(total[:, LAST, cols], centre[:, cols], largest[LAST][:, cols], ALU.add)
 
         out_rows = out.rearrange("(a p) v -> p a v", p=P)
-        halves = [slice(h * V_HALF, (h + 1) * V_HALF) for h in range(2)]
-        z_bf = keep.tile([P, V, LANES], BF16, name="z_bf", align_bytes=64)
-        for cols in halves:
-            nc.vector.tensor_tensor(larger[:, :, cols, :], edge_bf[0][:, :, cols, :], edge_bf[1][:, :, cols, :], ALU.max)
-        for cols in halves:
-            woven = [tile[:, :, cols, :].rearrange("p u v s -> p v u s") for tile in (larger, edge_bf[2])]
-            nc.vector.tensor_tensor(z_bf[:, cols, :].rearrange("p v (u s) -> p v u s", u=2), woven[0], woven[1], ALU.max)
+        z_bf = [keep.tile([P, V_HALF, LANES], BF16, name=f"z_bf{h}", align_bytes=64) for h in range(2)]
+        for h, cols in enumerate(CENTRE_HALVES):
+            nc.scalar.activation(z_bf[h][:, :, LOW], total[:, LOW, cols].rearrange("p t v -> p v t"), ACT.Relu)
+        for h, cols in enumerate(CENTRE_HALVES):
+            nc.vector.tensor_scalar_max(z_bf[h][:, :, HIGH], total[:, HIGH, cols].rearrange("p t v -> p v t"), 0.0)
 
-        def quantise_z(h):
-            codes = keep.tile([P, V_HALF], U32, name=f"z_codes{h}", align_bytes=64)
-            scale = keep.tile([P, V_HALF], U8, name=f"z_scale{h}", align_bytes=64)
-            nc.vector.quantize_mx(out=codes[:].bitcast(FP8X4), scales=scale[:], in_=z_bf[:, halves[h], :].rearrange("p v t -> p (v t)"))
-            return codes, scale
-
-        def project(dst, a, z_op):
-            nc.tensor.matmul_mx(
-                out=dst,
-                lhsT=w3_codes[:, 2 * P * a : 2 * P * (a + 1)].bitcast(FP4X4),
-                lhsT_scale=w3_scale[:, P * a : P * (a + 1)],
-                rhs=z_op[0][:].bitcast(FP8X4),
-                rhs_scale=z_op[1][:],
-                start=True,
-                stop=True,
-            )
-
-        for h, cols in enumerate(halves):
-            z_op = quantise_z(h)
+        for h, cols in enumerate(CENTRE_HALVES):
+            z_codes = keep.tile([P, V_HALF], U32, name=f"z_codes{h}", align_bytes=64)
+            z_scale = keep.tile([P, V_HALF], U8, name=f"z_scale{h}", align_bytes=64)
+            nc.vector.quantize_mx(out=z_codes[:].bitcast(FP8X4), scales=z_scale[:], in_=z_bf[h][:].rearrange("p v t -> p (v t)"))
             for a, (engine_copy, queue) in enumerate(((nc.vector.tensor_copy, nc.sync), (nc.scalar.copy, nc.scalar))):
-                out_bank = out_psum.tile([P, V_HALF], F32, name="out_bank")
-                project(out_bank[:], a, z_op)
+                out_bank = psum.tile([P, V_HALF], F32, name=f"out_bank{h}{a}", tag=f"bank{2 * h + a}")
+                nc.tensor.matmul_mx(
+                    out=out_bank[:],
+                    lhsT=w3_codes[:, 2 * P * a : 2 * P * (a + 1)].bitcast(FP4X4),
+                    lhsT_scale=w3_scale[:, P * a : P * (a + 1)],
+                    rhs=z_codes[:].bitcast(FP8X4),
+                    rhs_scale=z_scale[:],
+                    start=True,
+                    stop=True,
+                )
                 staged = keep.tile([P, V_HALF], F32, name=f"staged{h}{a}")
                 engine_copy(staged[:], out_bank[:])
                 queue.dma_start(out_rows[:, a, cols], staged[:])

@@ -26,6 +26,7 @@ V_HALF = V // 2
 ALL_POINTS = slice(0, S)
 POINT_HALVES = (slice(0, S_HALF), slice(S_HALF, S))
 CENTRE_HALVES = (slice(0, V_HALF), slice(V_HALF, V))
+Y_LAST_PIECES = (slice(0, S // 2), slice(S // 2, 3 * S // 4), slice(3 * S // 4, S))
 LOW, HIGH = slice(0, 2), slice(2, 4)
 X_FEW = 64
 W2_LEFT_SCALAR_PLACES = 24
@@ -120,17 +121,19 @@ def tile_picked_edgecv_relu_e_kernel(tc, xT, w1, w2, w3_words, w3_scales, offs, 
             nc.vector.quantize_mx(out=codes[:].bitcast(FP8X4), scales=scale[:], in_=w_bf[:].rearrange("p t m j -> p (t m j)"))
             return [(codes[:, i * P : (i + 1) * P], scale[:, i * P : (i + 1) * P]) for i in range(count)]
 
-        def product(weights, bank_no, cols):
-            bank = psum.tile([P, cols.stop - cols.start], F32, name=f"bank{bank_no}", tag=f"bank{bank_no}")
-            nc.tensor.matmul_mx(
-                out=bank[:],
-                lhsT=weights[0].bitcast(FP8X4),
-                lhsT_scale=weights[1],
-                rhs=x_codes[:, cols].bitcast(FP8X4),
-                rhs_scale=x_scale[:, cols],
-                start=True,
-                stop=True,
-            )
+        def product(weights, bank_no, *pieces):
+            first = pieces[0].start
+            bank = psum.tile([P, pieces[-1].stop - first], F32, name=f"bank{bank_no}", tag=f"bank{bank_no}")
+            for cols in pieces:
+                nc.tensor.matmul_mx(
+                    out=bank[:, cols.start - first : cols.stop - first],
+                    lhsT=weights[0].bitcast(FP8X4),
+                    lhsT_scale=weights[1],
+                    rhs=x_codes[:, cols].bitcast(FP8X4),
+                    rhs_scale=x_scale[:, cols],
+                    start=True,
+                    stop=True,
+                )
             return bank
 
         w2_bf = keep.tile([P, LANES, P, LANES], BF16, name="w2_bf", align_bytes=64)
@@ -148,10 +151,11 @@ def tile_picked_edgecv_relu_e_kernel(tc, xT, w1, w2, w3_words, w3_scales, offs, 
         w1_bf = place([P, LANES, P, LANES], BF16, "w1_bf", W1_BF_AT)
         w1_dst = w1_bf[:].rearrange("p t m j -> p m j t")
         nc.vector.tensor_copy(w1_dst[:, 0:W1_FIRST_PLACES], dealt(w1_first))
-        nc.vector.tensor_copy(w1_dst[:, W1_FIRST_PLACES:P], dealt(w1_last))
-        w1_ops = quantise(w1_bf, "w1")
+        for pair in (LOW, HIGH):
+            nc.vector.tensor_copy(w1_dst[:, W1_FIRST_PLACES:P, :, pair], dealt(w1_last)[:, :, :, pair])
+        w1_ops = quantise(w1_bf[:, LOW], "w1_low") + quantise(w1_bf[:, HIGH], "w1_high")
         y_banks = [product(w1_ops[t], Y_BANK + t, ALL_POINTS) for t in range(LAST)]
-        y_last_banks = [product(w1_ops[LAST], bank_no, cols) for cols, bank_no in zip(POINT_HALVES, (0, Y_BANK + LAST))]
+        y_last_banks = [product(w1_ops[LAST], 0, *Y_LAST_PIECES[:2]), product(w1_ops[LAST], Y_BANK + LAST, Y_LAST_PIECES[2])]
 
         e = e + [place([P, S], F32, f"e{t}", W1_FIRST_AT + (t - 2) * ROW_BYTES) for t in range(2, LANES)]
         y = [keep.tile([P, S], F32, name=f"y{t}") for t in range(LANES)]
@@ -187,9 +191,10 @@ def tile_picked_edgecv_relu_e_kernel(tc, xT, w1, w2, w3_words, w3_scales, offs, 
             nc.scalar.copy(e[t + 2][:], late_e_banks[t][:])
         for d in range(3):
             fetch(2, d, scalar_gather)
-        nc.scalar.copy(y[LAST][:, POINT_HALVES[0]], y_last_banks[0][:])
-        for d in range(3):
+        for d in range(2):
             fetch(LAST, d, scalar_gather)
+        nc.scalar.copy(y[LAST][:, 0 : Y_LAST_PIECES[1].stop], y_last_banks[0][:])
+        fetch(LAST, 2, scalar_gather)
         all_centres = slice(0, V)
         first_max(0)
         empty_y(0)
@@ -199,7 +204,7 @@ def tile_picked_edgecv_relu_e_kernel(tc, xT, w1, w2, w3_words, w3_scales, offs, 
         add_centre(0)
         second_max(1, all_centres)
         empty_y(2)
-        nc.vector.tensor_copy(y[LAST][:, POINT_HALVES[1]], y_last_banks[1][:])
+        nc.vector.tensor_copy(y[LAST][:, Y_LAST_PIECES[2]], y_last_banks[1][:])
         for cols in CENTRE_HALVES:
             scalar_gather(centre[:, cols], y[LAST][:].indirect(entries_of(cen_list, cols.start, cols.stop)))
         first_max(2)

@@ -151,9 +151,8 @@ def tile_picked_edgecv_relu_e_kernel(tc, xT, w1, w2, w3_words, w3_scales, offs, 
         w1_bf = place([P, LANES, P, LANES], BF16, "w1_bf", W1_BF_AT)
         w1_dst = w1_bf[:].rearrange("p t m j -> p m j t")
         nc.vector.tensor_copy(w1_dst[:, 0:W1_FIRST_PLACES], dealt(w1_first))
-        for pair in (LOW, HIGH):
-            nc.vector.tensor_copy(w1_dst[:, W1_FIRST_PLACES:P, :, pair], dealt(w1_last)[:, :, :, pair])
-        w1_ops = quantise(w1_bf[:, LOW], "w1_low") + quantise(w1_bf[:, HIGH], "w1_high")
+        nc.vector.tensor_copy(w1_dst[:, W1_FIRST_PLACES:P], dealt(w1_last))
+        w1_ops = quantise(w1_bf, "w1")
         y_banks = [product(w1_ops[t], Y_BANK + t, ALL_POINTS) for t in range(LAST)]
         y_last_banks = [product(w1_ops[LAST], 0, *Y_LAST_PIECES[:2]), product(w1_ops[LAST], Y_BANK + LAST, Y_LAST_PIECES[2])]
 
@@ -191,10 +190,9 @@ def tile_picked_edgecv_relu_e_kernel(tc, xT, w1, w2, w3_words, w3_scales, offs, 
             nc.scalar.copy(e[t + 2][:], late_e_banks[t][:])
         for d in range(3):
             fetch(2, d, scalar_gather)
-        for d in range(2):
-            fetch(LAST, d, scalar_gather)
         nc.scalar.copy(y[LAST][:, 0 : Y_LAST_PIECES[1].stop], y_last_banks[0][:])
-        fetch(LAST, 2, scalar_gather)
+        for d in range(3):
+            fetch(LAST, d, scalar_gather)
         all_centres = slice(0, V)
         first_max(0)
         empty_y(0)

@@ -29,6 +29,7 @@ CENTRE_HALVES = (slice(0, V_HALF), slice(V_HALF, V))
 Y_LAST_PIECES = (slice(0, S // 2), slice(S // 2, 3 * S // 4), slice(3 * S // 4, S))
 LOW, HIGH = slice(0, 2), slice(2, 4)
 X_FEW = 64
+X_SCALAR_HIGH = 64
 W2_LEFT_SCALAR_PLACES = 24
 W2_RIGHT_SCALAR_PLACES = 20
 W1_FIRST_PLACES = 96
@@ -39,6 +40,7 @@ W1_LAST_AT = W1_FIRST_AT + 4 * LANES * LANES * W1_FIRST_PLACES
 W1_BF_AT = W1_FIRST_AT + 4 * LANES * H
 LARGEST_AT = W1_BF_AT + 2 * LANES * H
 PICKED_AT = LARGEST_AT + LANES * CENTRE_BYTES
+X_LAST_AT = PICKED_AT + 4 * LANES * S_HALF
 Y_BANK = LANES
 
 
@@ -65,7 +67,7 @@ def tile_picked_edgecv_relu_e_kernel(tc, xT, w1, w2, w3_words, w3_scales, offs, 
             nc.scalar.activation(dst, window, ACT.Copy)
 
         x_rows = xT.rearrange("(p j) c -> p j c", j=LANES)
-        x_lane = [keep.tile([P, T], F32, name=f"x_lane{j}") for j in range(LANES)]
+        x_lane = [keep.tile([P, T], F32, name=f"x_lane{j}") for j in range(LAST)] + [place([P, T], F32, "x_lane_last", X_LAST_AT)]
         nc.sync.dma_start(x_lane[0][:], x_rows[:, 0, :])
         offs_list = load_list(offs, S, "offs_list")
         for j in range(1, LANES):
@@ -102,11 +104,14 @@ def tile_picked_edgecv_relu_e_kernel(tc, xT, w1, w2, w3_words, w3_scales, offs, 
             nc.vector.tensor_copy(x_bf[0][:, :, j], x_lane[j][:].indirect(entries_of(offs_list, 0, S_HALF)))
         for j in (1, 2):
             scalar_gather(picked[:, j, :], x_lane[j][:].indirect(entries_of(offs_list, S_HALF, S)))
+        nc.scalar.copy(x_bf[1][:, few, 1], picked[:, 1, few])
         nc.scalar.copy(x_bf[1][:, rest, LOW], picked[:, LOW, rest].rearrange("p j s -> p s j"))
-        scalar_gather(picked[:, LAST, :], x_lane[LAST][:].indirect(entries_of(offs_list, S_HALF, S)))
-        nc.vector.tensor_copy(x_bf[1][:, rest, HIGH], picked[:, HIGH, rest].rearrange("p j s -> p s j"))
-        nc.vector.tensor_copy(x_bf[1][:, few, 1:LANES], picked[:, 1:LANES, few].rearrange("p j s -> p s j"))
-        x_codes = keep.tile([P, S], U32, name="x_codes", align_bytes=64)
+        x_cut = S_HALF - X_SCALAR_HIGH
+        for start, stop in ((0, x_cut), (x_cut, S_HALF)):
+            scalar_gather(picked[:, LAST, start:stop], x_lane[LAST][:].indirect(entries_of(offs_list, S_HALF + start, S_HALF + stop)))
+        for points, copy in ((slice(0, x_cut), nc.vector.tensor_copy), (slice(x_cut, S_HALF), nc.scalar.copy)):
+            copy(x_bf[1][:, points, HIGH], picked[:, HIGH, points].rearrange("p j s -> p s j"))
+        x_codes = place([P, S], U32, "x_codes", X_LAST_AT)
         x_scale = keep.tile([P, S], U8, name="x_scale", align_bytes=64)
         for h, cols in enumerate(POINT_HALVES):
             nc.vector.quantize_mx(out=x_codes[:, cols].bitcast(FP8X4), scales=x_scale[:, cols], in_=x_bf[h][:].rearrange("p s j -> p (s j)"))
@@ -147,13 +152,13 @@ def tile_picked_edgecv_relu_e_kernel(tc, xT, w1, w2, w3_words, w3_scales, offs, 
         for t in range(2):
             for cols, bank_no in zip(POINT_HALVES, (t, Y_BANK + LAST - t)):
                 nc.scalar.copy(e[t][:, cols], product(w2_ops[t], bank_no, cols)[:])
-        late_e_banks = [product(w2_ops[t], t, ALL_POINTS) for t in range(2, LANES)]
+        late_e_banks = [product(w2_ops[t], bank_no, ALL_POINTS) for t, bank_no in ((2, Y_BANK + 2), (LAST, 1))]
         w1_bf = place([P, LANES, P, LANES], BF16, "w1_bf", W1_BF_AT)
         w1_dst = w1_bf[:].rearrange("p t m j -> p m j t")
         nc.vector.tensor_copy(w1_dst[:, 0:W1_FIRST_PLACES], dealt(w1_first))
         nc.vector.tensor_copy(w1_dst[:, W1_FIRST_PLACES:P], dealt(w1_last))
         w1_ops = quantise(w1_bf, "w1")
-        y_banks = [product(w1_ops[t], Y_BANK + t, ALL_POINTS) for t in range(LAST)]
+        y_banks = [product(w1_ops[t], bank_no, ALL_POINTS) for t, bank_no in enumerate((Y_BANK, Y_BANK + 1, 2))]
         y_last_banks = [product(w1_ops[LAST], 0, *Y_LAST_PIECES[:2]), product(w1_ops[LAST], Y_BANK + LAST, Y_LAST_PIECES[2])]
 
         e = e + [place([P, S], F32, f"e{t}", W1_FIRST_AT + (t - 2) * ROW_BYTES) for t in range(2, LANES)]

@@ -29,7 +29,6 @@ CENTRE_HALVES = (slice(0, V_HALF), slice(V_HALF, V))
 Y_LAST_PIECES = (slice(0, S // 2), slice(S // 2, 3 * S // 4), slice(3 * S // 4, S))
 LOW, HIGH = slice(0, 2), slice(2, 4)
 X_FEW = 64
-X_SCALAR_HIGH = 64
 W2_LEFT_SCALAR_PLACES = 24
 W2_RIGHT_SCALAR_PLACES = 20
 W1_FIRST_PLACES = 96
@@ -105,12 +104,10 @@ def tile_picked_edgecv_relu_e_kernel(tc, xT, w1, w2, w3_words, w3_scales, offs, 
         for j in (1, 2):
             scalar_gather(picked[:, j, :], x_lane[j][:].indirect(entries_of(offs_list, S_HALF, S)))
         nc.scalar.copy(x_bf[1][:, few, 1], picked[:, 1, few])
-        nc.scalar.copy(x_bf[1][:, rest, LOW], picked[:, LOW, rest].rearrange("p j s -> p s j"))
-        x_cut = S_HALF - X_SCALAR_HIGH
-        for start, stop in ((0, x_cut), (x_cut, S_HALF)):
-            scalar_gather(picked[:, LAST, start:stop], x_lane[LAST][:].indirect(entries_of(offs_list, S_HALF + start, S_HALF + stop)))
-        for points, copy in ((slice(0, x_cut), nc.vector.tensor_copy), (slice(x_cut, S_HALF), nc.scalar.copy)):
-            copy(x_bf[1][:, points, HIGH], picked[:, HIGH, points].rearrange("p j s -> p s j"))
+        for points in (rest, few):
+            scalar_gather(picked[:, LAST, points], x_lane[LAST][:].indirect(entries_of(offs_list, S_HALF + points.start, S_HALF + points.stop)))
+        nc.vector.tensor_copy(x_bf[1][:, rest, :].rearrange("p (c i) j -> p c j i", i=LANES), picked[:, :, rest].rearrange("p j (c i) -> p c j i", i=LANES))
+        nc.scalar.copy(x_bf[1][:, few, HIGH], picked[:, HIGH, few].rearrange("p j s -> p s j"))
         x_codes = place([P, S], U32, "x_codes", X_LAST_AT)
         x_scale = keep.tile([P, S], U8, name="x_scale", align_bytes=64)
         for h, cols in enumerate(POINT_HALVES):
@@ -223,9 +220,7 @@ def tile_picked_edgecv_relu_e_kernel(tc, xT, w1, w2, w3_words, w3_scales, offs, 
         out_rows = out.rearrange("(a p) v -> p a v", p=P)
         z_bf = [keep.tile([P, V_HALF, LANES], BF16, name=f"z_bf{h}", align_bytes=64) for h in range(2)]
         for h, cols in enumerate(CENTRE_HALVES):
-            nc.scalar.activation(z_bf[h][:, :, LOW], total[:, LOW, cols].rearrange("p t v -> p v t"), ACT.Relu)
-        for h, cols in enumerate(CENTRE_HALVES):
-            nc.vector.tensor_scalar_max(z_bf[h][:, :, HIGH], total[:, HIGH, cols].rearrange("p t v -> p v t"), 0.0)
+            nc.vector.tensor_scalar_max(z_bf[h][:].rearrange("p (c i) t -> p c t i", i=LANES), total[:, :, cols].rearrange("p t (c i) -> p c t i", i=LANES), 0.0)
 
         for h, cols in enumerate(CENTRE_HALVES):
             z_codes = keep.tile([P, V_HALF], U32, name=f"z_codes{h}", align_bytes=64)

from contextlib import ExitStack

import concourse.mybir as mybir

K, T, S, V, H, N = 512, 1024, 512, 256, 512, 256
FLOPS = 2 * (2 * K * H * S + H * N * V)

F32 = mybir.dt.float32
BF16 = mybir.dt.bfloat16
I32 = mybir.dt.int32
U32 = mybir.dt.uint32
U16 = mybir.dt.uint16
U8 = mybir.dt.uint8
FP8X4 = mybir.dt.float8_e4m3fn_x4
FP4X4 = mybir.dt.float4_e2m1fn_x4
ALU = mybir.AluOpType
ACT = mybir.ActivationFunctionType

P = 128
LANES = 4
LAST = LANES - 1
GROUP = 16
QUADRANT = 32
S_HALF = S // 2
V_HALF = V // 2
ALL_POINTS = slice(0, S)
POINT_HALVES = (slice(0, S_HALF), slice(S_HALF, S))
CENTRE_HALVES = (slice(0, V_HALF), slice(V_HALF, V))
Y_LAST_PIECES = (slice(0, S // 2), slice(S // 2, 3 * S // 4), slice(3 * S // 4, S))
LOW, HIGH = slice(0, 2), slice(2, 4)
X_FEW = 64
W2_LEFT_SCALAR_PLACES = 24
W2_RIGHT_SCALAR_PLACES = 20
W1_FIRST_PLACES = 96
ROW_BYTES = 4 * S
CENTRE_BYTES = 4 * V
W1_FIRST_AT = 0
W1_LAST_AT = W1_FIRST_AT + 4 * LANES * LANES * W1_FIRST_PLACES
W1_BF_AT = W1_FIRST_AT + 4 * LANES * H
LARGEST_AT = W1_BF_AT + 2 * LANES * H
PICKED_AT = LARGEST_AT + LANES * CENTRE_BYTES
X_LAST_AT = PICKED_AT + 4 * LANES * S_HALF
Y_BANK = LANES


def tile_picked_edgecv_relu_e_kernel(tc, xT, w1, w2, w3_words, w3_scales, offs, cen, pos1, pos2, pos3, out):
    nc = tc.nc
    with ExitStack() as ctx:
        lists = ctx.enter_context(tc.tile_pool(name="lists", bufs=1))
        keep = ctx.enter_context(tc.tile_pool(name="keep", bufs=1))
        placed = ctx.enter_context(tc.tile_pool(name="placed", bufs=1))
        psum = ctx.enter_context(tc.psum_pool(name="psum", bufs=1))

        def load_list(src, entries, name):
            tile = lists.tile([P, entries // GROUP], U16, name=name)
            nc.sync.dma_start(tile[:], src)
            return tile

        def entries_of(list_tile, start, stop):
            return list_tile[:, start // GROUP : stop // GROUP]

        def place(shape, dtype, name, offset):
            return placed.tile(shape, dtype, name=name, offset=offset, align_bytes=64)

        def scalar_gather(dst, window):
            nc.scalar.activation(dst, window, ACT.Copy)

        x_rows = xT.rearrange("(p j) c -> p j c", j=LANES)
        x_lane = [keep.tile([P, T], F32, name=f"x_lane{j}") for j in range(LAST)] + [place([P, T], F32, "x_lane_last", X_LAST_AT)]
        nc.sync.dma_start(x_lane[0][:], x_rows[:, 0, :])
        offs_list = load_list(offs, S, "offs_list")
        for j in range(1, LANES):
            nc.sync.dma_start(x_lane[j][:], x_rows[:, j, :])

        w2_raw = keep.tile([P, LANES, H], F32, name="w2_raw")
        w2_cut = LANES * H - H // 2
        for run in (slice(0, w2_cut), slice(w2_cut, LANES * H)):
            nc.sync.dma_start(w2_raw[:].rearrange("p j c -> p (j c)")[:, run], w2.rearrange("(p j) c -> p (j c)", j=LANES)[:, run])
        pos_lists = [load_list(src, V, f"pos_list{d}") for d, src in enumerate((pos1, pos2, pos3))]
        w1_rows = w1.rearrange("(p j) c -> p j c", j=LANES)
        w1_cut = LANES * W1_FIRST_PLACES
        w1_first = place([P, LANES, w1_cut], F32, "w1_first", W1_FIRST_AT)
        nc.sync.dma_start(w1_first[:], w1_rows[:, :, 0:w1_cut])
        w1_last = place([P, LANES, H - w1_cut], F32, "w1_last", W1_LAST_AT)
        nc.sync.dma_start(w1_last[:], w1_rows[:, :, w1_cut:H])
        cen_list = load_list(cen, V, "cen_list")

        w3_codes = keep.tile([P, 2 * N], U8, name="w3_codes", align_bytes=64)
        nc.sync.dma_start(w3_codes[:].bitcast(I32), w3_words[0].bitcast(I32))
        w3_scale = keep.tile([P, N], U8, name="w3_scale", align_bytes=64)
        nc.vector.memset(w3_scale[:].bitcast(I32), 0)
        for q in range(P // QUADRANT):
            nc.sync.dma_start(w3_scale[QUADRANT * q : QUADRANT * q + 4, :].bitcast(I32), w3_scales[0, 4 * q : 4 * q + 4, :].bitcast(I32))

        x_bf = [keep.tile([P, S_HALF, LANES], BF16, name=f"x_bf{h}", align_bytes=64) for h in range(2)]
        few, rest = slice(0, X_FEW), slice(X_FEW, S_HALF)
        picked = place([P, LANES, S_HALF], F32, "picked", PICKED_AT)
        first_few = place([P, X_FEW], F32, "first_few", PICKED_AT + 4 * X_FEW)
        nc.vector.tensor_copy(first_few[:], x_lane[0][:].indirect(entries_of(offs_list, S_HALF, S_HALF + X_FEW)))
        nc.scalar.copy(x_bf[1][:, few, 0], first_few[:])
        scalar_gather(picked[:, 0, rest], x_lane[0][:].indirect(entries_of(offs_list, S_HALF + X_FEW, S)))
        for j in range(LANES):
            nc.vector.tensor_copy(x_bf[0][:, :, j], x_lane[j][:].indirect(entries_of(offs_list, 0, S_HALF)))
        for j in (1, 2):
            scalar_gather(picked[:, j, :], x_lane[j][:].indirect(entries_of(offs_list, S_HALF, S)))
        nc.scalar.copy(x_bf[1][:, few, 1], picked[:, 1, few])
        for points in (rest, few):
            scalar_gather(picked[:, LAST, points], x_lane[LAST][:].indirect(entries_of(offs_list, S_HALF + points.start, S_HALF + points.stop)))
        nc.vector.tensor_copy(x_bf[1][:, rest, :].rearrange("p (c i) j -> p c j i", i=LANES), picked[:, :, rest].rearrange("p j (c i) -> p c j i", i=LANES))
        nc.scalar.copy(x_bf[1][:, few, HIGH], picked[:, HIGH, few].rearrange("p j s -> p s j"))
        x_codes = place([P, S], U32, "x_codes", X_LAST_AT)
        x_scale = keep.tile([P, S], U8, name="x_scale", align_bytes=64)
        for h, cols in enumerate(POINT_HALVES):
            nc.vector.quantize_mx(out=x_codes[:, cols].bitcast(FP8X4), scales=x_scale[:, cols], in_=x_bf[h][:].rearrange("p s j -> p (s j)"))

        def dealt(raw):
            return raw[:].rearrange("p j (m t) -> p m j t", t=LANES)

        def quantise(w_bf, name):
            count = w_bf.shape[1]
            codes = keep.tile([P, count * P], U32, name=f"{name}_codes", align_bytes=64)
            scale = keep.tile([P, count * P], U8, name=f"{name}_scale", align_bytes=64)
            nc.vector.quantize_mx(out=codes[:].bitcast(FP8X4), scales=scale[:], in_=w_bf[:].rearrange("p t m j -> p (t m j)"))
            return [(codes[:, i * P : (i + 1) * P], scale[:, i * P : (i + 1) * P]) for i in range(count)]

        def product(weights, bank_no, *pieces):
            first = pieces[0].start
            bank = psum.tile([P, pieces[-1].stop - first], F32, name=f"bank{bank_no}", tag=f"bank{bank_no}")
            for cols in pieces:
                nc.tensor.matmul_mx(
                    out=bank[:, cols.start - first : cols.stop - first],
                    lhsT=weights[0].bitcast(FP8X4),
                    lhsT_scale=weights[1],
                    rhs=x_codes[:, cols].bitcast(FP8X4),
                    rhs_scale=x_scale[:, cols],
                    start=True,
                    stop=True,
                )
            return bank

        w2_bf = keep.tile([P, LANES, P, LANES], BF16, name="w2_bf", align_bytes=64)
        w2_dst = w2_bf[:].rearrange("p t m j -> p m j t")
        for start, scalar_places in ((0, W2_LEFT_SCALAR_PLACES), (P // 2, W2_RIGHT_SCALAR_PLACES)):
            cut, stop = start + scalar_places, start + P // 2
            nc.scalar.copy(w2_dst[:, start:cut], dealt(w2_raw)[:, start:cut])
            nc.vector.tensor_copy(w2_dst[:, cut:stop], dealt(w2_raw)[:, cut:stop])
        w2_ops = quantise(w2_bf[:, 0:1], "w2_first") + quantise(w2_bf[:, 1:LANES], "w2_rest")
        e = [keep.tile([P, S], F32, name=f"e{t}") for t in range(2)]
        for t in range(2):
            for cols, bank_no in zip(POINT_HALVES, (t, Y_BANK + LAST - t)):
                nc.scalar.copy(e[t][:, cols], product(w2_ops[t], bank_no, cols)[:])
        late_e_banks = [product(w2_ops[t], bank_no, ALL_POINTS) for t, bank_no in ((2, Y_BANK + 2), (LAST, 1))]
        w1_bf = place([P, LANES, P, LANES], BF16, "w1_bf", W1_BF_AT)
        w1_dst = w1_bf[:].rearrange("p t m j -> p m j t")
        nc.vector.tensor_copy(w1_dst[:, 0:W1_FIRST_PLACES], dealt(w1_first))
        nc.vector.tensor_copy(w1_dst[:, W1_FIRST_PLACES:P], dealt(w1_last))
        w1_ops = quantise(w1_bf, "w1")
        y_banks = [product(w1_ops[t], bank_no, ALL_POINTS) for t, bank_no in enumerate((Y_BANK, Y_BANK + 1, 2))]
        y_last_banks = [product(w1_ops[LAST], 0, *Y_LAST_PIECES[:2]), product(w1_ops[LAST], Y_BANK + LAST, Y_LAST_PIECES[2])]

        e = e + [place([P, S], F32, f"e{t}", W1_FIRST_AT + (t - 2) * ROW_BYTES) for t in range(2, LANES)]
        y = [keep.tile([P, S], F32, name=f"y{t}") for t in range(LANES)]
        near = [[keep.tile([P, V], F32, name=f"near{t}{d}") for d in range(2)] for t in range(LANES)]
        for t in range(LANES):
            name = f"near{t}2"
            near[t].append(place([P, V], F32, name, W1_LAST_AT + t * CENTRE_BYTES) if t < 2 else keep.tile([P, V], F32, name=name))
        larger = [place([P, V], F32, f"larger{t}", (W1_BF_AT if t < 2 else LARGEST_AT) + (t % 2) * CENTRE_BYTES) for t in range(LANES)]
        largest = [place([P, V], F32, f"largest{t}", LARGEST_AT + t * CENTRE_BYTES) for t in range(LANES)]
        centre = keep.tile([P, V], F32, name="centre")
        total = keep.tile([P, LANES, V], F32, name="total")

        def fetch(t, d, gather):
            gather(near[t][d][:], e[t][:].indirect(pos_lists[d][:]))

        def first_max(t):
            nc.vector.tensor_tensor(larger[t][:], near[t][0][:], near[t][1][:], ALU.max)

        def second_max(t, cols):
            nc.vector.tensor_tensor(largest[t][:, cols], larger[t][:, cols], near[t][2][:, cols], ALU.max)

        def empty_y(t):
            nc.vector.tensor_copy(y[t][:], y_banks[t][:])

        def add_centre(t):
            nc.vector.tensor_tensor(total[:, t, :], y[t][:].indirect(cen_list[:]), largest[t][:], ALU.add)

        for t in range(2):
            fetch(t, 2, nc.vector.tensor_copy)
        for t in range(2):
            for d in range(2):
                fetch(t, d, scalar_gather)
            nc.scalar.copy(e[t + 2][:], late_e_banks[t][:])
        for d in range(3):
            fetch(2, d, scalar_gather)
        nc.scalar.copy(y[LAST][:, 0 : Y_LAST_PIECES[1].stop], y_last_banks[0][:])
        for d in range(3):
            fetch(LAST, d, scalar_gather)
        all_centres = slice(0, V)
        first_max(0)
        empty_y(0)
        second_max(0, all_centres)
        empty_y(1)
        first_max(1)
        add_centre(0)
        second_max(1, all_centres)
        empty_y(2)
        nc.vector.tensor_copy(y[LAST][:, Y_LAST_PIECES[2]], y_last_banks[1][:])
        for cols in CENTRE_HALVES:
            scalar_gather(centre[:, cols], y[LAST][:].indirect(entries_of(cen_list, cols.start, cols.stop)))
        first_max(2)
        add_centre(1)
        second_max(2, all_centres)
        first_max(LAST)
        add_centre(2)
        for cols in CENTRE_HALVES:
            second_max(LAST, cols)
        for cols in CENTRE_HALVES:
            nc.vector.tensor_tensor(total[:, LAST, cols], centre[:, cols], largest[LAST][:, cols], ALU.add)

        out_rows = out.rearrange("(a p) v -> p a v", p=P)
        z_bf = [keep.tile([P, V_HALF, LANES], BF16, name=f"z_bf{h}", align_bytes=64) for h in range(2)]
        for h, cols in enumerate(CENTRE_HALVES):
            nc.vector.tensor_scalar_max(z_bf[h][:].rearrange("p (c i) t -> p c t i", i=LANES), total[:, :, cols].rearrange("p t (c i) -> p c t i", i=LANES), 0.0)

        for h, cols in enumerate(CENTRE_HALVES):
            z_codes = keep.tile([P, V_HALF], U32, name=f"z_codes{h}", align_bytes=64)
            z_scale = keep.tile([P, V_HALF], U8, name=f"z_scale{h}", align_bytes=64)
            nc.vector.quantize_mx(out=z_codes[:].bitcast(FP8X4), scales=z_scale[:], in_=z_bf[h][:].rearrange("p v t -> p (v t)"))
            for a, (engine_copy, queue) in enumerate(((nc.vector.tensor_copy, nc.sync), (nc.scalar.copy, nc.scalar))):
                out_bank = psum.tile([P, V_HALF], F32, name=f"out_bank{h}{a}", tag=f"bank{2 * h + a}")
                nc.tensor.matmul_mx(
                    out=out_bank[:],
                    lhsT=w3_codes[:, 2 * P * a : 2 * P * (a + 1)].bitcast(FP4X4),
                    lhsT_scale=w3_scale[:, P * a : P * (a + 1)],
                    rhs=z_codes[:].bitcast(FP8X4),
                    rhs_scale=z_scale[:],
                    start=True,
                    stop=True,
                )
                staged = keep.tile([P, V_HALF], F32, name=f"staged{h}{a}")
                engine_copy(staged[:], out_bank[:])
                queue.dma_start(out_rows[:, a, cols], staged[:])
